import numpy as np
import ml_dtypes


def mxq(x, axis, fmt="e4m3"):
    dtype, down = {"e4m3": (ml_dtypes.float8_e4m3fn, 7), "e5m2": (ml_dtypes.float8_e5m2, 14)}[fmt]
    v = np.moveaxis(np.asarray(x, np.float32).astype(ml_dtypes.bfloat16).astype(np.float64), axis, -1)
    blocks = v.reshape(v.shape[:-1] + (-1, 32))
    amax = np.abs(blocks).max(-1, keepdims=True)
    byte = np.maximum(np.where(amax > 0, np.frexp(amax)[1] - 1 + 127, 0) - down, 1)
    scale = np.exp2(byte - 127.0)
    codes = (blocks / scale).astype(np.float32).astype(dtype).astype(np.float64)
    return np.moveaxis((codes * scale).reshape(v.shape), -1, axis)


WIDE = False


def mx_kscale(k):
    if not WIDE:
        return np.ones(k)
    levels = np.array([10, -10, 5, -5, 0])
    if k % 512:
        return np.exp2(np.random.permutation(np.resize(levels, k // 32))).repeat(32)
    a = np.empty((k // 512, 16))
    for p in range(k // 512):
        a[p, :8] = np.random.permutation(np.resize(levels, 8))
        for g in range(8):
            far = levels[np.abs(levels - a[p, g]) >= 10]
            a[p, g + 8] = far[np.random.randint(len(far))]
    return np.exp2(a.ravel()).repeat(32)


def f64(x):
    return np.asarray(x).astype(np.float64)


def striped(idx):
    return np.tile(idx.reshape(-1, 16).T, (8, 1)).astype(np.uint16)


def unstriped(offs):
    return offs[:16].T.reshape(-1).astype(np.int64)


def striped8(idx):
    return np.concatenate([x.reshape(-1, 16).T for x in idx]).astype(np.uint16)


def runs(offs, k):
    lists = np.stack([offs[16 * r : 16 * r + 16].T.reshape(-1) for r in range(8)]).astype(np.int64)
    return lists[np.arange(k) % 512 // 64]


def pack_weight(w):
    k, n = w.shape
    w = f64(np.asarray(w, np.float32).astype(ml_dtypes.bfloat16)).reshape(k // 32, 32, n)
    amax = np.abs(w).max(1)
    byte = np.clip(np.where(amax > 0, np.frexp(amax)[1] - 1 + 127 - 7, 1), 1, 254)
    scaled = (w * np.exp2(127.0 - byte)[:, None, :]).reshape(k, n).astype(np.float32)
    words = np.ascontiguousarray(scaled.reshape(k // 512, 128, 4, n).transpose(0, 1, 3, 2)).astype(ml_dtypes.float8_e4m3fn).view(np.uint8)
    return words, np.ascontiguousarray(byte.astype(np.uint8).reshape(k // 512, 16, n))


def unpack_weight(words, scales):
    g, p, n, _ = words.shape
    vals = np.ascontiguousarray(words).view(ml_dtypes.float8_e4m3fn).astype(np.float64) * np.repeat(np.exp2(scales.astype(np.float64) - 127.0), 8, axis=1)[..., None]
    return vals.transpose(0, 1, 3, 2).reshape(g * 512, n)


def relu(v):
    return np.maximum(v, 0.0)

def planes(y):
    n, m = y.shape
    v = y.astype(np.float32).astype(ml_dtypes.bfloat16).astype(np.float64).reshape(n // 32, 32, m)
    top = np.abs(v).max(1)
    byte = np.clip(np.where(top > 0, np.frexp(top)[1] - 1 + 127 - 7, 1), 1, 254)
    codes = (v * np.exp2(127.0 - byte)[:, None, :]).reshape(n, m).astype(np.float32).astype(ml_dtypes.float8_e4m3fn).view(np.uint8)
    words = codes.reshape(n // 512, 128, 4, m).transpose(0, 1, 3, 2)
    return np.ascontiguousarray(words), np.ascontiguousarray(byte.astype(np.uint8).reshape(n // 512, 16, m))


K, T, S, V, N, H = 512, 2048, 1024, 512, 512, 512


def setup_inputs():
    n = np.random.standard_normal
    s = mx_kscale(K)[:, None]
    u = mx_kscale(H)
    packed_xT = pack_weight(n((K, T)) * s)
    packed_w3 = pack_weight(n((H, N)) / np.sqrt(H) / u[:, None])
    return {
        "x_words": packed_xT[0],
        "x_scales": packed_xT[1],
        "w1": (n((K, H)) / np.sqrt(K) / s * u).astype(np.float32),
        "w2": (n((H, H)) / np.sqrt(H) / u[:, None] * u).astype(np.float32),
        "res": (2 * n((N, S))).astype(np.float32),
        "w3_words": packed_w3[0],
        "w3_scales": packed_w3[1],
        "offs": striped(np.random.permutation(T)[:S]),
        "order": striped8(np.stack([np.random.permutation(S) for _ in range(8)])),
        "par": striped8(np.random.randint(0, V, (8, S))),
    }


def reference(x_words, x_scales, w1, w2, res, w3_words, w3_scales, offs, order, par):
    xq = unpack_weight(x_words, x_scales)[:, unstriped(offs)]
    y = relu(mxq(f64(w1), 0, "e4m3").T @ xq)
    o = y[np.arange(H)[:, None], runs(order, H)]
    z = o.reshape(H, V, 2).max(axis=2)
    h = relu(mxq(f64(w2), 0, "e4m3").T @ mxq(z, 0, "e4m3"))
    z2 = y + h[np.arange(H)[:, None], runs(par, H)]
    out_0 = f64(res) + (unpack_weight(w3_words, w3_scales).T @ mxq(z2, 0, "e4m3"))
    return (out_0,) + planes(out_0)

@@ -1,0 +1,175 @@
+from contextlib import ExitStack
+
+import concourse.mybir as mybir
+
+K, T, S, V, N, H = 512, 2048, 1024, 512, 512, 512
+FLOPS = 2 * K * H * S + 2 * H * H * V + 2 * H * N * S
+
+F32 = mybir.dt.float32
+BF16 = mybir.dt.bfloat16
+I32 = mybir.dt.int32
+U32 = mybir.dt.uint32
+U16 = mybir.dt.uint16
+U8 = mybir.dt.uint8
+FP8X4 = mybir.dt.float8_e4m3fn_x4
+RELU = mybir.ActivationFunctionType.Relu
+COPY = mybir.ActivationFunctionType.Copy
+ADD = mybir.AluOpType.add
+MAX = mybir.AluOpType.max
+
+P = 128
+PACK = 4
+LANES = 16
+BANK = 512
+PICK_PIECES = (512, 256, 256)
+POOL_PIECES = (512, 256, 256)
+FINE_PIECES = (256, 256, 256, 128, 128)
+
+
+def spans(widths):
+    return [(sum(widths[:i]), sum(widths[: i + 1])) for i in range(len(widths))]
+
+
+def tile_picked_unet1_relu_po_kernel(
+    tc, x_words, x_scales, w1, w2, res, w3_words, w3_scales, offs, order, par, out_0, out_1, out_2
+):
+    nc = tc.nc
+    with ExitStack() as ctx:
+        lists = ctx.enter_context(tc.tile_pool(name="lists", bufs=1))
+        keep = ctx.enter_context(tc.tile_pool(name="keep", bufs=1))
+        ring = ctx.enter_context(tc.tile_pool(name="ring", bufs=2))
+        psum = ctx.enter_context(tc.psum_pool(name="psum", bufs=8))
+
+        def load_list(source, name):
+            held = lists.tile([P, S // LANES], U16, name=name)
+            nc.sync.dma_start(held[:], source)
+            return held
+
+        def entries(held, a, b):
+            return held[:, a // LANES : b // LANES]
+
+        def load_scale_rows(source, width, name, queue):
+            plane = keep.tile([P, width], U8, name=name, tag="scale_rows", align_bytes=64)
+            nc.vector.memset(plane[:].bitcast(I32), 0)
+            for q in range(4):
+                queue.dma_start(plane[32 * q : 32 * q + 4, :].bitcast(I32), source[0, 4 * q : 4 * q + 4, :].bitcast(I32))
+            return plane
+
+        def load_weight_half(w, u, name):
+            raw = keep.tile([P, PACK, H // 2], F32, name="%s_raw%d" % (name, u), tag="weight_raw%d" % u)
+            nc.sync.dma_start(raw[:], w.rearrange("(p j) c -> p j c", j=PACK)[:, :, u * H // 2 : (u + 1) * H // 2])
+            return raw
+
+        def quantise_weight(halves, name):
+            rounded = keep.tile([P, PACK, P, PACK], BF16, name=name + "_rounded", tag="rounded", align_bytes=64)
+            for u, raw in enumerate(halves):
+                nc.scalar.activation(
+                    rounded[:, :, u * P // 2 : (u + 1) * P // 2, :].rearrange("p t m j -> p m t j"),
+                    raw[:].rearrange("p j (m t) -> p m t j", t=PACK),
+                    COPY,
+                )
+            codes = keep.tile([P, H], U32, name=name + "_codes", align_bytes=64)
+            scales = keep.tile([P, H], U8, name=name + "_scales", align_bytes=64)
+            nc.vector.quantize_mx(codes[:].bitcast(FP8X4), scales[:], rounded[:].rearrange("p t m j -> p (t m j)"))
+            return codes, scales
+
+        def product(w_codes, w_scales, codes, scales, width):
+            per_bank = BANK // width
+            banks = []
+            for t0 in range(0, PACK, per_bank):
+                bank = psum.tile([P, per_bank, width], F32, name="bank")
+                for i in range(per_bank):
+                    cols = slice((t0 + i) * P, (t0 + i + 1) * P)
+                    nc.tensor.matmul_mx(bank[:, i, :], w_codes[:, cols].bitcast(FP8X4), w_scales[:, cols], codes.bitcast(FP8X4), scales, start=True, stop=True)
+                banks.append((t0, per_bank, bank))
+            return banks
+
+        def relu_into(planes, banks, a, b):
+            for t0, count, bank in banks:
+                for i in range(count):
+                    nc.scalar.activation(planes[t0 + i][:, a:b], bank[:, i, :], RELU)
+
+        def round_interleaved(values, width, name):
+            rounded = ring.tile([P, width * PACK], BF16, name=name, align_bytes=64)
+            nc.scalar.activation(
+                rounded[:].rearrange("p (c i t) -> p c t i", i=4, t=PACK),
+                values[:].rearrange("p t (c i) -> p c t i", i=4),
+                COPY,
+            )
+            return rounded
+
+        offs_t = load_list(offs, "offs_t")
+        w1_low = load_weight_half(w1, 0, "w1")
+        x_rows = load_scale_rows(x_scales, T, "x_rows", nc.sync)
+        w1_high = load_weight_half(w1, 1, "w1")
+        x_table = keep.tile([P, T], U32, name="x_table", tag="wide")
+        nc.sync.dma_start(x_table[:].bitcast(I32), x_words[0].rearrange("p n r -> p (n r)").bitcast(I32))
+        order_t = load_list(order, "order_t")
+        par_t = load_list(par, "par_t")
+
+        picked_scales = keep.tile([P, S], U8, name="picked_scales", align_bytes=64)
+        nc.vector.tensor_copy(picked_scales[:], x_rows[:].indirect(offs_t[:]))
+        w1_codes, w1_scales = quantise_weight([w1_low, w1_high], "w1")
+        picked = []
+        for a, b in spans(PICK_PIECES):
+            words = keep.tile([P, b - a], U32, name="picked_words%d" % a, tag="scale_rows" if a == 0 else "picked%d" % a, align_bytes=64)
+            nc.vector.tensor_copy(words[:], x_table[:].indirect(entries(offs_t, a, b)))
+            picked.append(words)
+
+        y = [keep.tile([P, S], F32, name="y%d" % t) for t in range(PACK)]
+        for t in range(PACK):
+            cols = slice(t * P, (t + 1) * P)
+            for words, (a, b) in zip(picked, spans(PICK_PIECES)):
+                bank = psum.tile([P, b - a], F32, name="bank")
+                nc.tensor.matmul_mx(bank[:], w1_codes[:, cols].bitcast(FP8X4), w1_scales[:, cols], words[:].bitcast(FP8X4), picked_scales[:, a:b], start=True, stop=True)
+                nc.scalar.activation(y[t][:, a:b], bank[:], RELU)
+
+        w2_codes, w2_scales = quantise_weight([load_weight_half(w2, u, "w2") for u in range(2)], "w2")
+        w3_raw = keep.tile([P, N], U32, name="w3_raw", tag="weight_raw1")
+        nc.sync.dma_start(w3_raw[:].bitcast(I32), w3_words[0].rearrange("p n r -> p (n r)").bitcast(I32))
+        w3_rows = load_scale_rows(w3_scales, N, "w3_rows", nc.sync)
+        residual = keep.tile([P, PACK, S], F32, name="residual", tag="wide")
+        nc.sync.dma_start(residual[:], res.rearrange("(p t) j -> p t j", t=PACK))
+
+        h = [keep.tile([P, V], F32, name="h%d" % t) for t in range(PACK)]
+        for a, b in spans(POOL_PIECES):
+            width = (b - a) // 2
+            ordered = keep.tile([P, PACK, b - a], F32, name="ordered%d" % a, tag="rounded" if b == S else "ordered%d" % a, align_bytes=64)
+            for t in range(PACK):
+                nc.vector.tensor_copy(ordered[:, t, :], y[t][:].indirect(entries(order_t, a, b)))
+            pairs = ordered[:].rearrange("p t (c i e) -> p c t i e", i=2, e=2)
+            z = keep.tile([P, width * PACK], BF16, name="z%d" % a, align_bytes=64)
+            nc.vector.tensor_tensor(z[:].rearrange("p (c i t) -> p c t i", i=2, t=PACK), pairs[:, :, :, :, 0], pairs[:, :, :, :, 1], MAX)
+            z_codes = ring.tile([P, width], U32, name="z_codes", align_bytes=64)
+            z_scales = ring.tile([P, width], U8, name="z_scales", align_bytes=64)
+            nc.vector.quantize_mx(z_codes[:].bitcast(FP8X4), z_scales[:], z[:])
+            relu_into(h, product(w2_codes, w2_scales, z_codes[:], z_scales[:], width), a // 2, b // 2)
+
+        w3_codes = keep.tile([P, N], U32, name="w3_codes", tag="z768", align_bytes=64)
+        w3_planes = keep.tile([P, N], U8, name="w3_planes", tag="rounded", align_bytes=64)
+        nc.vector.tensor_copy(w3_codes[:].rearrange("p (t m) -> p t m", t=PACK), w3_raw[:].rearrange("p (m t) -> p t m", t=PACK))
+        nc.vector.tensor_copy(w3_planes[:].rearrange("p (t m) -> p t m", t=PACK), w3_rows[:].rearrange("p (m t) -> p t m", t=PACK))
+
+        out_rows = out_0.rearrange("(p t) j -> p t j", t=PACK)
+        out_words = out_1[0].rearrange("p n r -> p (n r)").bitcast(I32)
+        out_scales = keep.tile([P, S], U8, name="out_scales", align_bytes=64)
+        for a, b in spans(FINE_PIECES):
+            width = b - a
+            z2 = ring.tile([P, PACK, width], F32, name="z2")
+            for t in range(PACK):
+                nc.vector.tensor_tensor(z2[:, t, :], h[t][:].indirect(entries(par_t, a, b)), y[t][:, a:b], ADD)
+            z2_rounded = round_interleaved(z2, width, "z2_rounded")
+            z2_codes = ring.tile([P, width], U32, name="z2_codes", align_bytes=64)
+            z2_scales = ring.tile([P, width], U8, name="z2_scales", align_bytes=64)
+            nc.vector.quantize_mx(z2_codes[:].bitcast(FP8X4), z2_scales[:], z2_rounded[:])
+            result = ring.tile([P, PACK, width], F32, name="result", bufs=3)
+            for t0, count, bank in product(w3_codes, w3_planes, z2_codes[:], z2_scales[:], width):
+                nc.vector.tensor_tensor(result[:, t0 : t0 + count, :], bank[:], residual[:, t0 : t0 + count, a:b], ADD)
+            nc.sync.dma_start(out_rows[:, :, a:b], result[:])
+            result_rounded = round_interleaved(result, width, "result_rounded")
+            result_codes = ring.tile([P, width], U32, name="result_codes", align_bytes=64, bufs=3)
+            nc.vector.quantize_mx(result_codes[:].bitcast(FP8X4), out_scales[:, a:b], result_rounded[:])
+            nc.sync.dma_start(out_words[:, a:b], result_codes[:].bitcast(I32))
+        for q in range(4):
+            queue = nc.sync if q < 2 else nc.scalar
+            queue.dma_start(out_2[0, 4 * q : 4 * q + 4, :].bitcast(I32), out_scales[32 * q : 32 * q + 4, :].bitcast(I32))

@@ -22,8 +22,9 @@ PACK = 4
 LANES = 16
 BANK = 512
 PICK_PIECES = (512, 256, 256)
-POOL_PIECES = (512, 256, 256)
+POOL_PIECES = (512, 512)
 FINE_PIECES = (256, 256, 256, 128, 128)
+WORD_PIECES = (512, 384, 128)
 
 
 def spans(widths):
@@ -49,7 +50,7 @@ def tile_picked_unet1_relu_po_kernel(
             return held[:, a // LANES : b // LANES]
 
         def load_scale_rows(source, width, name, queue):
-            plane = keep.tile([P, width], U8, name=name, tag="scale_rows", align_bytes=64)
+            plane = keep.tile([P, width], U8, name=name, align_bytes=64)
             nc.vector.memset(plane[:].bitcast(I32), 0)
             for q in range(4):
                 queue.dma_start(plane[32 * q : 32 * q + 4, :].bitcast(I32), source[0, 4 * q : 4 * q + 4, :].bitcast(I32))
@@ -60,21 +61,21 @@ def tile_picked_unet1_relu_po_kernel(
             nc.sync.dma_start(raw[:], w.rearrange("(p j) c -> p j c", j=PACK)[:, :, u * H // 2 : (u + 1) * H // 2])
             return raw
 
-        def quantise_weight(halves, name):
-            rounded = keep.tile([P, PACK, P, PACK], BF16, name=name + "_rounded", tag="rounded", align_bytes=64)
+        def round_weight(halves, rounded):
             for u, raw in enumerate(halves):
                 nc.scalar.activation(
                     rounded[:, :, u * P // 2 : (u + 1) * P // 2, :].rearrange("p t m j -> p m t j"),
                     raw[:].rearrange("p j (m t) -> p m t j", t=PACK),
                     COPY,
                 )
-            codes = keep.tile([P, H], U32, name=name + "_codes", align_bytes=64)
-            scales = keep.tile([P, H], U8, name=name + "_scales", align_bytes=64)
-            nc.vector.quantize_mx(codes[:].bitcast(FP8X4), scales[:], rounded[:].rearrange("p t m j -> p (t m j)"))
+
+        def quantise_weight(rounded, width, name, tag):
+            codes = keep.tile([P, width], U32, name=name + "_codes", tag=tag, align_bytes=64)
+            scales = keep.tile([P, width], U8, name=name + "_scales", align_bytes=64)
+            nc.vector.quantize_mx(codes[:].bitcast(FP8X4), scales[:], rounded.rearrange("p t m j -> p (t m j)"))
             return codes, scales
 
-        def product(w_codes, w_scales, codes, scales, width):
-            per_bank = BANK // width
+        def product(w_codes, w_scales, codes, scales, width, per_bank):
             banks = []
             for t0 in range(0, PACK, per_bank):
                 bank = psum.tile([P, per_bank, width], F32, name="bank")
@@ -84,66 +85,89 @@ def tile_picked_unet1_relu_po_kernel(
                 banks.append((t0, per_bank, bank))
             return banks
 
-        def relu_into(planes, banks, a, b):
-            for t0, count, bank in banks:
-                for i in range(count):
-                    nc.scalar.activation(planes[t0 + i][:, a:b], bank[:, i, :], RELU)
-
-        def round_interleaved(values, width, name):
-            rounded = ring.tile([P, width * PACK], BF16, name=name, align_bytes=64)
-            nc.scalar.activation(
-                rounded[:].rearrange("p (c i t) -> p c t i", i=4, t=PACK),
-                values[:].rearrange("p t (c i) -> p c t i", i=4),
-                COPY,
-            )
+        def round_interleaved(values, width, name, on_vector=False):
+            rounded = ring.tile([P, width * PACK], BF16, name=name, align_bytes=64, bufs=5 if name == "result_rounded" else 2)
+            target = rounded[:].rearrange("p (c i t) -> p c t i", i=4, t=PACK)
+            source = values[:].rearrange("p t (c i) -> p c t i", i=4)
+            if on_vector:
+                nc.vector.tensor_copy(target, source)
+            else:
+                nc.scalar.activation(target, source, COPY)
             return rounded
 
         offs_t = load_list(offs, "offs_t")
         w1_low = load_weight_half(w1, 0, "w1")
         x_rows = load_scale_rows(x_scales, T, "x_rows", nc.sync)
         w1_high = load_weight_half(w1, 1, "w1")
-        x_table = keep.tile([P, T], U32, name="x_table", tag="wide")
+        x_table = keep.tile([P, T], U32, name="x_table", tag="wide", align_bytes=64)
         nc.sync.dma_start(x_table[:].bitcast(I32), x_words[0].rearrange("p n r -> p (n r)").bitcast(I32))
         order_t = load_list(order, "order_t")
         par_t = load_list(par, "par_t")
 
         picked_scales = keep.tile([P, S], U8, name="picked_scales", align_bytes=64)
         nc.vector.tensor_copy(picked_scales[:], x_rows[:].indirect(offs_t[:]))
-        w1_codes, w1_scales = quantise_weight([w1_low, w1_high], "w1")
+        w1_rounded = keep.tile([P, PACK, P, PACK], BF16, name="w1_rounded", tag="rounded", align_bytes=64)
+        round_weight([w1_low, w1_high], w1_rounded[:])
+        w1_pairs = [quantise_weight(w1_rounded[:, 0:2], 2 * P, "w1_first", "w1_first")]
         picked = []
         for a, b in spans(PICK_PIECES):
-            words = keep.tile([P, b - a], U32, name="picked_words%d" % a, tag="scale_rows" if a == 0 else "picked%d" % a, align_bytes=64)
+            words = keep.tile([P, b - a], U32, name="picked_words%d" % a, tag="x_rows" if a == 0 else "picked%d" % a, align_bytes=64)
             nc.vector.tensor_copy(words[:], x_table[:].indirect(entries(offs_t, a, b)))
             picked.append(words)
+        w1_pairs.append(quantise_weight(w1_rounded[:, 2:4], 2 * P, "w1_second", "wide"))
 
         y = [keep.tile([P, S], F32, name="y%d" % t) for t in range(PACK)]
         for t in range(PACK):
-            cols = slice(t * P, (t + 1) * P)
+            cols = slice(t % 2 * P, (t % 2 + 1) * P)
+            w1_codes, w1_scales = w1_pairs[t // 2]
             for words, (a, b) in zip(picked, spans(PICK_PIECES)):
                 bank = psum.tile([P, b - a], F32, name="bank")
                 nc.tensor.matmul_mx(bank[:], w1_codes[:, cols].bitcast(FP8X4), w1_scales[:, cols], words[:].bitcast(FP8X4), picked_scales[:, a:b], start=True, stop=True)
                 nc.scalar.activation(y[t][:, a:b], bank[:], RELU)
 
-        w2_codes, w2_scales = quantise_weight([load_weight_half(w2, u, "w2") for u in range(2)], "w2")
+        late = keep.tile([P, PACK + 1, S // 2], F32, name="late", tag="rounded", align_bytes=64)
+        w2_rounded = late[:, 3:5, :].rearrange("p a c -> p (a c)").bitcast(BF16).rearrange("p (t m j) -> p t m j", t=PACK, j=PACK)
+        round_weight([load_weight_half(w2, u, "w2") for u in range(2)], w2_rounded)
+        w2_codes, w2_scales = quantise_weight(w2_rounded, H, "w2", "w2_codes")
         w3_raw = keep.tile([P, N], U32, name="w3_raw", tag="weight_raw1")
         nc.sync.dma_start(w3_raw[:].bitcast(I32), w3_words[0].rearrange("p n r -> p (n r)").bitcast(I32))
         w3_rows = load_scale_rows(w3_scales, N, "w3_rows", nc.sync)
-        residual = keep.tile([P, PACK, S], F32, name="residual", tag="wide")
+        residual = keep.tile([P, PACK, S], F32, name="residual", tag="wide", align_bytes=64)
         nc.sync.dma_start(residual[:], res.rearrange("(p t) j -> p t j", t=PACK))
 
         h = [keep.tile([P, V], F32, name="h%d" % t) for t in range(PACK)]
         for a, b in spans(POOL_PIECES):
             width = (b - a) // 2
-            ordered = keep.tile([P, PACK, b - a], F32, name="ordered%d" % a, tag="rounded" if b == S else "ordered%d" % a, align_bytes=64)
+            if b == S:
+                ordered = late[:, :PACK, :]
+            else:
+                early = keep.tile([P, PACK, b - a], F32, name="early")
+                ordered = early[:]
             for t in range(PACK):
                 nc.vector.tensor_copy(ordered[:, t, :], y[t][:].indirect(entries(order_t, a, b)))
-            pairs = ordered[:].rearrange("p t (c i e) -> p c t i e", i=2, e=2)
-            z = keep.tile([P, width * PACK], BF16, name="z%d" % a, align_bytes=64)
-            nc.vector.tensor_tensor(z[:].rearrange("p (c i t) -> p c t i", i=2, t=PACK), pairs[:, :, :, :, 0], pairs[:, :, :, :, 1], MAX)
             z_codes = ring.tile([P, width], U32, name="z_codes", align_bytes=64)
             z_scales = ring.tile([P, width], U8, name="z_scales", align_bytes=64)
-            nc.vector.quantize_mx(z_codes[:].bitcast(FP8X4), z_scales[:], z[:])
-            relu_into(h, product(w2_codes, w2_scales, z_codes[:], z_scales[:], width), a // 2, b // 2)
+            parts = spans((P, P) if b == S else (width,))
+            zs = []
+            for c, d in parts:
+                pairs = ordered[:, :, 2 * c : 2 * d].rearrange("p t (c i e) -> p c t i e", i=2, e=2)
+                if a == 0:
+                    z = late[:, PACK, :].bitcast(BF16)
+                else:
+                    own = keep.tile([P, (d - c) * PACK], BF16, name="z%d" % (a + 2 * c), align_bytes=64)
+                    z = own[:]
+                nc.vector.tensor_tensor(z.rearrange("p (c i t) -> p c t i", i=2, t=PACK), pairs[:, :, :, :, 0], pairs[:, :, :, :, 1], MAX)
+                zs.append(z)
+            for (c, d), z in zip(parts, zs):
+                nc.vector.quantize_mx(z_codes[:, c:d].bitcast(FP8X4), z_scales[:, c:d], z)
+            for t in range(PACK):
+                cols = slice(t * P, (t + 1) * P)
+                for group in ([[part] for part in parts] if t == 0 else [parts]):
+                    lo, hi = group[0][0], group[-1][1]
+                    bank = psum.tile([P, hi - lo], F32, name="bank")
+                    for c, d in group:
+                        nc.tensor.matmul_mx(bank[:, c - lo : d - lo], w2_codes[:, cols].bitcast(FP8X4), w2_scales[:, cols], z_codes[:, c:d].bitcast(FP8X4), z_scales[:, c:d], start=True, stop=True)
+                    nc.scalar.activation(h[t][:, a // 2 + lo : a // 2 + hi], bank[:], RELU)
 
         w3_codes = keep.tile([P, N], U32, name="w3_codes", tag="z768", align_bytes=64)
         w3_planes = keep.tile([P, N], U8, name="w3_planes", tag="rounded", align_bytes=64)
@@ -153,7 +177,11 @@ def tile_picked_unet1_relu_po_kernel(
         out_rows = out_0.rearrange("(p t) j -> p t j", t=PACK)
         out_words = out_1[0].rearrange("p n r -> p (n r)").bitcast(I32)
         out_scales = keep.tile([P, S], U8, name="out_scales", align_bytes=64)
-        for a, b in spans(FINE_PIECES):
+
+        result_codes = keep.tile([P, S], U32, name="result_codes", align_bytes=64)
+        word_starts = {b: a for a, b in spans(WORD_PIECES)}
+
+        def front(a, b):
             width = b - a
             z2 = ring.tile([P, PACK, width], F32, name="z2")
             for t in range(PACK):
@@ -162,14 +190,25 @@ def tile_picked_unet1_relu_po_kernel(
             z2_codes = ring.tile([P, width], U32, name="z2_codes", align_bytes=64)
             z2_scales = ring.tile([P, width], U8, name="z2_scales", align_bytes=64)
             nc.vector.quantize_mx(z2_codes[:].bitcast(FP8X4), z2_scales[:], z2_rounded[:])
-            result = ring.tile([P, PACK, width], F32, name="result", bufs=3)
-            for t0, count, bank in product(w3_codes, w3_planes, z2_codes[:], z2_scales[:], width):
+            return product(w3_codes, w3_planes, z2_codes[:], z2_scales[:], width, 2 if b == S else BANK // width)
+
+        def back(a, b, banks):
+            width = b - a
+            result = ring.tile([P, PACK, width], F32, name="result", bufs=5)
+            for t0, count, bank in banks:
                 nc.vector.tensor_tensor(result[:, t0 : t0 + count, :], bank[:], residual[:, t0 : t0 + count, a:b], ADD)
             nc.sync.dma_start(out_rows[:, :, a:b], result[:])
-            result_rounded = round_interleaved(result, width, "result_rounded")
-            result_codes = ring.tile([P, width], U32, name="result_codes", align_bytes=64, bufs=3)
-            nc.vector.quantize_mx(result_codes[:].bitcast(FP8X4), out_scales[:, a:b], result_rounded[:])
-            nc.sync.dma_start(out_words[:, a:b], result_codes[:].bitcast(I32))
+            result_rounded = round_interleaved(result, width, "result_rounded", b == S)
+            nc.vector.quantize_mx(result_codes[:, a:b].bitcast(FP8X4), out_scales[:, a:b], result_rounded[:])
+            if b in word_starts:
+                nc.sync.dma_start(out_words[:, word_starts[b] : b], result_codes[:, word_starts[b] : b].bitcast(I32))
+
+        pieces = spans(FINE_PIECES)
+        banks = front(*pieces[0])
+        for k, piece in enumerate(pieces):
+            ahead = front(*pieces[k + 1]) if k + 1 < len(pieces) else None
+            back(*piece, banks)
+            banks = ahead
         for q in range(4):
             queue = nc.sync if q < 2 else nc.scalar
             queue.dma_start(out_2[0, 4 * q : 4 * q + 4, :].bitcast(I32), out_scales[32 * q : 32 * q + 4, :].bitcast(I32))

@@ -95,38 +95,49 @@ def tile_picked_unet1_relu_po_kernel(
                 nc.scalar.activation(target, source, COPY)
             return rounded
 
-        offs_t = load_list(offs, "offs_t")
         w1_low = load_weight_half(w1, 0, "w1")
+        offs_t = load_list(offs, "offs_t")
         x_rows = load_scale_rows(x_scales, T, "x_rows", nc.sync)
-        w1_high = load_weight_half(w1, 1, "w1")
         x_table = keep.tile([P, T], U32, name="x_table", tag="wide", align_bytes=64)
         nc.sync.dma_start(x_table[:].bitcast(I32), x_words[0].rearrange("p n r -> p (n r)").bitcast(I32))
+        w1_high = load_weight_half(w1, 1, "w1")
         order_t = load_list(order, "order_t")
         par_t = load_list(par, "par_t")
 
         picked_scales = keep.tile([P, S], U8, name="picked_scales", align_bytes=64)
         nc.vector.tensor_copy(picked_scales[:], x_rows[:].indirect(offs_t[:]))
-        w1_rounded = keep.tile([P, PACK, P, PACK], BF16, name="w1_rounded", tag="rounded", align_bytes=64)
-        round_weight([w1_low, w1_high], w1_rounded[:])
-        w1_pairs = [quantise_weight(w1_rounded[:, 0:2], 2 * P, "w1_first", "w1_first")]
+        first_rounded = keep.tile([P, 1, P, PACK], BF16, name="first_rounded", align_bytes=64)
+        other_rounded = keep.tile([P, PACK - 1, P, PACK], BF16, name="other_rounded", tag="rounded", align_bytes=64)
+        for u, raw in enumerate((w1_low, w1_high)):
+            source = raw[:].rearrange("p j (m t) -> p m t j", t=PACK)
+            rows = slice(u * P // 2, (u + 1) * P // 2)
+            nc.scalar.activation(first_rounded[:, :, rows, :].rearrange("p t m j -> p m t j"), source[:, :, :1, :], COPY)
+            nc.scalar.activation(other_rounded[:, :, rows, :].rearrange("p t m j -> p m t j"), source[:, :, 1:, :], COPY)
+        w1_planes = [quantise_weight(first_rounded[:], P, "w1_first", "w1_first") + (0,)]
         picked = []
         for a, b in spans(PICK_PIECES):
-            words = keep.tile([P, b - a], U32, name="picked_words%d" % a, tag="x_rows" if a == 0 else "picked%d" % a, align_bytes=64)
+            tag = "x_rows" if a == 0 else ("first_rounded" if b == S else "picked%d" % a)
+            words = keep.tile([P, b - a], U32, name="picked_words%d" % a, tag=tag, align_bytes=64)
             nc.vector.tensor_copy(words[:], x_table[:].indirect(entries(offs_t, a, b)))
             picked.append(words)
-        w1_pairs.append(quantise_weight(w1_rounded[:, 2:4], 2 * P, "w1_second", "wide"))
+        w1_planes.append(quantise_weight(other_rounded[:, :1], P, "w1_second", "w1_second") + (0,))
+        last_pair = quantise_weight(other_rounded[:, 1:], 2 * P, "w1_last", "w1_last")
+        w1_planes.extend([last_pair + (0,), last_pair + (P,)])
 
-        y = [keep.tile([P, S], F32, name="y%d" % t) for t in range(PACK)]
-        for t in range(PACK):
-            cols = slice(t % 2 * P, (t % 2 + 1) * P)
-            w1_codes, w1_scales = w1_pairs[t // 2]
-            for words, (a, b) in zip(picked, spans(PICK_PIECES)):
+        y = [keep.tile([P, 2 * S], F32, name="y%d" % t) for t in range(PACK)]
+        for t, (w1_codes, w1_scales, start) in enumerate(w1_planes):
+            cols = slice(start, start + P)
+            for i, (words, (a, b)) in enumerate(zip(picked, spans(PICK_PIECES))):
                 bank = psum.tile([P, b - a], F32, name="bank")
                 nc.tensor.matmul_mx(bank[:], w1_codes[:, cols].bitcast(FP8X4), w1_scales[:, cols], words[:].bitcast(FP8X4), picked_scales[:, a:b], start=True, stop=True)
-                nc.scalar.activation(y[t][:, a:b], bank[:], RELU)
+                if t == 0 and i == 1:
+                    nc.vector.tensor_scalar_max(y[t][:, a:b], bank[:], 0.0)
+                else:
+                    nc.scalar.activation(y[t][:, a:b], bank[:], RELU)
 
-        late = keep.tile([P, PACK + 1, S // 2], F32, name="late", tag="rounded", align_bytes=64)
-        w2_rounded = late[:, 3:5, :].rearrange("p a c -> p (a c)").bitcast(BF16).rearrange("p (t m j) -> p t m j", t=PACK, j=PACK)
+        late = keep.tile([P, PACK * S + S // 2], F32, name="late", tag="rounded", align_bytes=64)
+        ordered_all = late[:, : PACK * S].rearrange("p (t c) -> p t c", t=PACK)
+        w2_rounded = late[:, PACK * S - S // 2 :].bitcast(BF16).rearrange("p (t m j) -> p t m j", t=PACK, j=PACK)
         round_weight([load_weight_half(w2, u, "w2") for u in range(2)], w2_rounded)
         w2_codes, w2_scales = quantise_weight(w2_rounded, H, "w2", "w2_codes")
         w3_raw = keep.tile([P, N], U32, name="w3_raw", tag="weight_raw1")
@@ -136,15 +147,12 @@ def tile_picked_unet1_relu_po_kernel(
         nc.sync.dma_start(residual[:], res.rearrange("(p t) j -> p t j", t=PACK))
 
         h = [keep.tile([P, V], F32, name="h%d" % t) for t in range(PACK)]
+        for t in range(PACK - 1):
+            nc.vector.tensor_copy(ordered_all[:, t, :], y[t][:].indirect(order_t[:]))
         for a, b in spans(POOL_PIECES):
             width = (b - a) // 2
-            if b == S:
-                ordered = late[:, :PACK, :]
-            else:
-                early = keep.tile([P, PACK, b - a], F32, name="early")
-                ordered = early[:]
-            for t in range(PACK):
-                nc.vector.tensor_copy(ordered[:, t, :], y[t][:].indirect(entries(order_t, a, b)))
+            ordered = ordered_all[:, :, a:b]
+            nc.vector.tensor_copy(ordered[:, PACK - 1, :], y[PACK - 1][:].indirect(entries(order_t, a, b)))
             z_codes = ring.tile([P, width], U32, name="z_codes", align_bytes=64)
             z_scales = ring.tile([P, width], U8, name="z_scales", align_bytes=64)
             parts = spans((P, P) if b == S else (width,))
@@ -152,7 +160,7 @@ def tile_picked_unet1_relu_po_kernel(
             for c, d in parts:
                 pairs = ordered[:, :, 2 * c : 2 * d].rearrange("p t (c i e) -> p c t i e", i=2, e=2)
                 if a == 0:
-                    z = late[:, PACK, :].bitcast(BF16)
+                    z = late[:, PACK * S :].bitcast(BF16)
                 else:
                     own = keep.tile([P, (d - c) * PACK], BF16, name="z%d" % (a + 2 * c), align_bytes=64)
                     z = own[:]

@@ -21,8 +21,9 @@ P = 128
 PACK = 4
 LANES = 16
 BANK = 512
+OVERLAP = 64
 PICK_PIECES = (512, 256, 256)
-POOL_PIECES = (512, 512)
+POOL_PIECES = (512, 256, 256)
 FINE_PIECES = (256, 256, 256, 128, 128)
 WORD_PIECES = (512, 384, 128)
 
@@ -61,13 +62,12 @@ def tile_picked_unet1_relu_po_kernel(
             nc.sync.dma_start(raw[:], w.rearrange("(p j) c -> p j c", j=PACK)[:, :, u * H // 2 : (u + 1) * H // 2])
             return raw
 
-        def round_weight(halves, rounded):
-            for u, raw in enumerate(halves):
-                nc.scalar.activation(
-                    rounded[:, :, u * P // 2 : (u + 1) * P // 2, :].rearrange("p t m j -> p m t j"),
-                    raw[:].rearrange("p j (m t) -> p m t j", t=PACK),
-                    COPY,
-                )
+        def round_weight_half(raw, u, rounded):
+            nc.scalar.activation(
+                rounded[:, :, u * P // 2 : (u + 1) * P // 2, :].rearrange("p t m j -> p m t j"),
+                raw[:].rearrange("p j (m t) -> p m t j", t=PACK),
+                COPY,
+            )
 
         def quantise_weight(rounded, width, name, tag):
             codes = keep.tile([P, width], U32, name=name + "_codes", tag=tag, align_bytes=64)
@@ -116,7 +116,7 @@ def tile_picked_unet1_relu_po_kernel(
         w1_planes = [quantise_weight(first_rounded[:], P, "w1_first", "w1_first") + (0,)]
         picked = []
         for a, b in spans(PICK_PIECES):
-            tag = "x_rows" if a == 0 else ("first_rounded" if b == S else "picked%d" % a)
+            tag = "first_rounded" if b == S else "picked%d" % a
             words = keep.tile([P, b - a], U32, name="picked_words%d" % a, tag=tag, align_bytes=64)
             nc.vector.tensor_copy(words[:], x_table[:].indirect(entries(offs_t, a, b)))
             picked.append(words)
@@ -124,7 +124,7 @@ def tile_picked_unet1_relu_po_kernel(
         last_pair = quantise_weight(other_rounded[:, 1:], 2 * P, "w1_last", "w1_last")
         w1_planes.extend([last_pair + (0,), last_pair + (P,)])
 
-        y = [keep.tile([P, 2 * S], F32, name="y%d" % t) for t in range(PACK)]
+        y = [keep.tile([P, S if t == PACK - 1 else 2 * S], F32, name="y%d" % t) for t in range(PACK)]
         for t, (w1_codes, w1_scales, start) in enumerate(w1_planes):
             cols = slice(start, start + P)
             for i, (words, (a, b)) in enumerate(zip(picked, spans(PICK_PIECES))):
@@ -135,12 +135,12 @@ def tile_picked_unet1_relu_po_kernel(
                 else:
                     nc.scalar.activation(y[t][:, a:b], bank[:], RELU)
 
-        late = keep.tile([P, PACK * S + S // 2], F32, name="late", tag="rounded", align_bytes=64)
-        ordered_all = late[:, : PACK * S].rearrange("p (t c) -> p t c", t=PACK)
-        w2_rounded = late[:, PACK * S - S // 2 :].bitcast(BF16).rearrange("p (t m j) -> p t m j", t=PACK, j=PACK)
-        round_weight([load_weight_half(w2, u, "w2") for u in range(2)], w2_rounded)
-        w2_codes, w2_scales = quantise_weight(w2_rounded, H, "w2", "w2_codes")
-        w3_raw = keep.tile([P, N], U32, name="w3_raw", tag="weight_raw1")
+        late = keep.tile([P, (PACK + 1) * S - OVERLAP], F32, name="late", tag="rounded", align_bytes=64)
+        ordered_all = late[:, S - OVERLAP :].rearrange("p (t c) -> p t c", t=PACK)
+        w2_rounded = late[:, :S].bitcast(BF16).rearrange("p (t m j) -> p t m j", t=PACK, j=PACK)
+        w2_halves = [load_weight_half(w2, u, "w2") for u in range(2)]
+        round_weight_half(w2_halves[0], 0, w2_rounded)
+        w3_raw = keep.tile([P, N], U32, name="w3_raw", tag="weight_raw0")
         nc.sync.dma_start(w3_raw[:].bitcast(I32), w3_words[0].rearrange("p n r -> p (n r)").bitcast(I32))
         w3_rows = load_scale_rows(w3_scales, N, "w3_rows", nc.sync)
         residual = keep.tile([P, PACK, S], F32, name="residual", tag="wide", align_bytes=64)
@@ -149,38 +149,61 @@ def tile_picked_unet1_relu_po_kernel(
         h = [keep.tile([P, V], F32, name="h%d" % t) for t in range(PACK)]
         for t in range(PACK - 1):
             nc.vector.tensor_copy(ordered_all[:, t, :], y[t][:].indirect(order_t[:]))
-        for a, b in spans(POOL_PIECES):
-            width = (b - a) // 2
-            ordered = ordered_all[:, :, a:b]
-            nc.vector.tensor_copy(ordered[:, PACK - 1, :], y[PACK - 1][:].indirect(entries(order_t, a, b)))
-            z_codes = ring.tile([P, width], U32, name="z_codes", align_bytes=64)
-            z_scales = ring.tile([P, width], U8, name="z_scales", align_bytes=64)
-            parts = spans((P, P) if b == S else (width,))
-            zs = []
-            for c, d in parts:
-                pairs = ordered[:, :, 2 * c : 2 * d].rearrange("p t (c i e) -> p c t i e", i=2, e=2)
-                if a == 0:
-                    z = late[:, PACK * S :].bitcast(BF16)
-                else:
-                    own = keep.tile([P, (d - c) * PACK], BF16, name="z%d" % (a + 2 * c), align_bytes=64)
-                    z = own[:]
-                nc.vector.tensor_tensor(z.rearrange("p (c i t) -> p c t i", i=2, t=PACK), pairs[:, :, :, :, 0], pairs[:, :, :, :, 1], MAX)
-                zs.append(z)
-            for (c, d), z in zip(parts, zs):
-                nc.vector.quantize_mx(z_codes[:, c:d].bitcast(FP8X4), z_scales[:, c:d], z)
-            for t in range(PACK):
-                cols = slice(t * P, (t + 1) * P)
-                for group in ([[part] for part in parts] if t == 0 else [parts]):
-                    lo, hi = group[0][0], group[-1][1]
-                    bank = psum.tile([P, hi - lo], F32, name="bank")
-                    for c, d in group:
-                        nc.tensor.matmul_mx(bank[:, c - lo : d - lo], w2_codes[:, cols].bitcast(FP8X4), w2_scales[:, cols], z_codes[:, c:d].bitcast(FP8X4), z_scales[:, c:d], start=True, stop=True)
-                    nc.scalar.activation(h[t][:, a // 2 + lo : a // 2 + hi], bank[:], RELU)
+        def gather_last_plane(a, b):
+            nc.vector.tensor_copy(ordered_all[:, PACK - 1, a:b], y[PACK - 1][:].indirect(entries(order_t, a, b)))
 
-        w3_codes = keep.tile([P, N], U32, name="w3_codes", tag="z768", align_bytes=64)
-        w3_planes = keep.tile([P, N], U8, name="w3_planes", tag="rounded", align_bytes=64)
+        def part_pairs(u, a, b):
+            nc.scalar.activation(
+                parted[a][:, :, u, :, :],
+                ordered_all[:, 2 * u : 2 * u + 2, a:b].rearrange("p s (c e) -> p e c s", e=2),
+                COPY,
+            )
+
+        def largest_parted(a, b, name):
+            z = keep.tile([P, (b - a) // 2 * PACK], BF16, name=name, align_bytes=64)
+            sides = [parted[a][:, e].rearrange("p u c s -> p c u s") for e in range(2)]
+            nc.vector.tensor_tensor(z[:].rearrange("p (c u s) -> p c u s", u=2, s=2), sides[0], sides[1], MAX)
+            return z
+
+        z_codes = keep.tile([P, V], U32, name="z_codes", align_bytes=64)
+        z_scales = keep.tile([P, V], U8, name="z_scales", align_bytes=64)
+
+        def quantise_z(z, a, b):
+            nc.vector.quantize_mx(z_codes[:, a // 2 : b // 2].bitcast(FP8X4), z_scales[:, a // 2 : b // 2], z[:])
+
+        def coarse_product(t, a, b):
+            cols = slice(t * P, (t + 1) * P)
+            coarse = slice(a // 2, b // 2)
+            bank = psum.tile([P, (b - a) // 2], F32, name="bank")
+            nc.tensor.matmul_mx(bank[:], w2_codes[:, cols].bitcast(FP8X4), w2_scales[:, cols], z_codes[:, coarse].bitcast(FP8X4), z_scales[:, coarse], start=True, stop=True)
+            if (t, a) == (PACK - 1, 0):
+                nc.vector.tensor_scalar_max(h[t][:, coarse], bank[:], 0.0)
+            else:
+                nc.scalar.activation(h[t][:, coarse], bank[:], RELU)
+
+        first, second, last = spans(POOL_PIECES)
+        parted = {}
+        for (a, b), tag in zip((first, second, last), ("first_rounded", "picked_scales", "w1_last")):
+            parted[a] = keep.tile([P, 2, 2, (b - a) // 2, 2], BF16, name="parted%d" % a, tag=tag, align_bytes=64)
+            part_pairs(0, a, b)
+        round_weight_half(w2_halves[1], 1, w2_rounded)
+        for piece in (first, second, last):
+            gather_last_plane(*piece)
+            part_pairs(1, *piece)
+        w2_codes, w2_scales = quantise_weight(w2_rounded, H, "w2", "w2_codes")
+        z_first = largest_parted(*first, "z_first")
+        z_second = largest_parted(*second, "z_second")
+        quantise_z(z_first, *first)
+        z_last = largest_parted(*last, "z_last")
+        quantise_z(z_second, *second)
+        w3_codes = keep.tile([P, N], U32, name="w3_codes", tag="z_first", align_bytes=64)
         nc.vector.tensor_copy(w3_codes[:].rearrange("p (t m) -> p t m", t=PACK), w3_raw[:].rearrange("p (m t) -> p t m", t=PACK))
+        quantise_z(z_last, *last)
+        w3_planes = keep.tile([P, N], U8, name="w3_planes", tag="z_second", align_bytes=64)
         nc.vector.tensor_copy(w3_planes[:].rearrange("p (t m) -> p t m", t=PACK), w3_rows[:].rearrange("p (m t) -> p t m", t=PACK))
+        rest = (second[0], S)
+        for t, piece in ((0, first), (1, first), (0, second), (2, first), (3, first), (0, last), (1, rest), (2, rest), (3, rest)):
+            coarse_product(t, *piece)
 
         out_rows = out_0.rearrange("(p t) j -> p t j", t=PACK)
         out_words = out_1[0].rearrange("p n r -> p (n r)").bitcast(I32)

@@ -21,7 +21,7 @@ P = 128
 PACK = 4
 LANES = 16
 BANK = 512
-OVERLAP = 64
+LAST_PLANE_PIECES = (256, 256, 256, 256)
 PICK_PIECES = (512, 256, 256)
 POOL_PIECES = (512, 256, 256)
 FINE_PIECES = (256, 256, 256, 128, 128)
@@ -64,8 +64,8 @@ def tile_picked_unet1_relu_po_kernel(
 
         def round_weight_half(raw, u, rounded):
             nc.scalar.activation(
-                rounded[:, :, u * P // 2 : (u + 1) * P // 2, :].rearrange("p t m j -> p m t j"),
-                raw[:].rearrange("p j (m t) -> p m t j", t=PACK),
+                rounded[:, :, u * P // 2 : (u + 1) * P // 2, :].rearrange("p t m j -> p m j t"),
+                raw[:].rearrange("p j (m t) -> p m j t", t=PACK),
                 COPY,
             )
 
@@ -135,11 +135,13 @@ def tile_picked_unet1_relu_po_kernel(
                 else:
                     nc.scalar.activation(y[t][:, a:b], bank[:], RELU)
 
-        late = keep.tile([P, (PACK + 1) * S - OVERLAP], F32, name="late", tag="rounded", align_bytes=64)
-        ordered_all = late[:, S - OVERLAP :].rearrange("p (t c) -> p t c", t=PACK)
+        late = keep.tile([P, (PACK + 1) * S], F32, name="late", tag="rounded", align_bytes=64)
+        ordered_all = late[:, S:].rearrange("p (t c) -> p t c", t=PACK)
         w2_rounded = late[:, :S].bitcast(BF16).rearrange("p (t m j) -> p t m j", t=PACK, j=PACK)
         w2_halves = [load_weight_half(w2, u, "w2") for u in range(2)]
-        round_weight_half(w2_halves[0], 0, w2_rounded)
+        for u, raw in enumerate(w2_halves):
+            round_weight_half(raw, u, w2_rounded)
+        w2_pairs = [quantise_weight(w2_rounded[:, :2], 2 * P, "w2_low", "w2_low")]
         w3_raw = keep.tile([P, N], U32, name="w3_raw", tag="weight_raw0")
         nc.sync.dma_start(w3_raw[:].bitcast(I32), w3_words[0].rearrange("p n r -> p (n r)").bitcast(I32))
         w3_rows = load_scale_rows(w3_scales, N, "w3_rows", nc.sync)
@@ -153,10 +155,11 @@ def tile_picked_unet1_relu_po_kernel(
             nc.vector.tensor_copy(ordered_all[:, PACK - 1, a:b], y[PACK - 1][:].indirect(entries(order_t, a, b)))
 
         def part_pairs(u, a, b):
-            nc.scalar.activation(
-                parted[a][:, :, u, :, :],
-                ordered_all[:, 2 * u : 2 * u + 2, a:b].rearrange("p s (c e) -> p e c s", e=2),
-                COPY,
+            start = max(first for first in parted if first <= a)
+            target = parted[start][:, :, u, (a - start) // 2 : (b - start) // 2, :]
+            nc.scalar.copy(
+                target.rearrange("p e (c i) s -> p c s i e", i=4),
+                ordered_all[:, 2 * u : 2 * u + 2, a:b].rearrange("p s (c i e) -> p c s i e", i=4, e=2),
             )
 
         def largest_parted(a, b, name):
@@ -165,6 +168,8 @@ def tile_picked_unet1_relu_po_kernel(
             nc.vector.tensor_tensor(z[:].rearrange("p (c u s) -> p c u s", u=2, s=2), sides[0], sides[1], MAX)
             return z
 
+        zero_bias = keep.tile([P, 1], F32, name="zero_bias")
+        nc.vector.memset(zero_bias[:], 0.0)
         z_codes = keep.tile([P, V], U32, name="z_codes", align_bytes=64)
         z_scales = keep.tile([P, V], U8, name="z_scales", align_bytes=64)
 
@@ -172,12 +177,15 @@ def tile_picked_unet1_relu_po_kernel(
             nc.vector.quantize_mx(z_codes[:, a // 2 : b // 2].bitcast(FP8X4), z_scales[:, a // 2 : b // 2], z[:])
 
         def coarse_product(t, a, b):
-            cols = slice(t * P, (t + 1) * P)
+            w2_codes, w2_scales = w2_pairs[t // 2]
+            cols = slice(t % 2 * P, (t % 2 + 1) * P)
             coarse = slice(a // 2, b // 2)
             bank = psum.tile([P, (b - a) // 2], F32, name="bank")
             nc.tensor.matmul_mx(bank[:], w2_codes[:, cols].bitcast(FP8X4), w2_scales[:, cols], z_codes[:, coarse].bitcast(FP8X4), z_scales[:, coarse], start=True, stop=True)
             if (t, a) == (PACK - 1, 0):
                 nc.vector.tensor_scalar_max(h[t][:, coarse], bank[:], 0.0)
+            elif t == PACK - 1:
+                nc.scalar.activation(h[t][:, coarse], bank[:], RELU, bias=zero_bias[:])
             else:
                 nc.scalar.activation(h[t][:, coarse], bank[:], RELU)
 
@@ -186,23 +194,22 @@ def tile_picked_unet1_relu_po_kernel(
         for (a, b), tag in zip((first, second, last), ("first_rounded", "picked_scales", "w1_last")):
             parted[a] = keep.tile([P, 2, 2, (b - a) // 2, 2], BF16, name="parted%d" % a, tag=tag, align_bytes=64)
             part_pairs(0, a, b)
-        round_weight_half(w2_halves[1], 1, w2_rounded)
-        for piece in (first, second, last):
+        for piece in spans(LAST_PLANE_PIECES):
             gather_last_plane(*piece)
             part_pairs(1, *piece)
-        w2_codes, w2_scales = quantise_weight(w2_rounded, H, "w2", "w2_codes")
         z_first = largest_parted(*first, "z_first")
         z_second = largest_parted(*second, "z_second")
         quantise_z(z_first, *first)
         z_last = largest_parted(*last, "z_last")
+        w2_pairs.append(quantise_weight(w2_rounded[:, 2:], 2 * P, "w2_high", "z_first"))
         quantise_z(z_second, *second)
-        w3_codes = keep.tile([P, N], U32, name="w3_codes", tag="z_first", align_bytes=64)
-        nc.vector.tensor_copy(w3_codes[:].rearrange("p (t m) -> p t m", t=PACK), w3_raw[:].rearrange("p (m t) -> p t m", t=PACK))
         quantise_z(z_last, *last)
-        w3_planes = keep.tile([P, N], U8, name="w3_planes", tag="z_second", align_bytes=64)
-        nc.vector.tensor_copy(w3_planes[:].rearrange("p (t m) -> p t m", t=PACK), w3_rows[:].rearrange("p (m t) -> p t m", t=PACK))
+        w3_codes = keep.tile([P, N], U32, name="w3_codes", tag="z_second", align_bytes=64)
+        nc.vector.tensor_copy(w3_codes[:].rearrange("p (t m) -> p m t", t=PACK), w3_raw[:].rearrange("p (m t) -> p m t", t=PACK))
+        w3_planes = keep.tile([P, N], U8, name="w3_planes", tag="z_last", align_bytes=64)
+        nc.vector.tensor_copy(w3_planes[:].rearrange("p (t m) -> p m t", t=PACK), w3_rows[:].rearrange("p (m t) -> p m t", t=PACK))
         rest = (second[0], S)
-        for t, piece in ((0, first), (1, first), (0, second), (2, first), (3, first), (0, last), (1, rest), (2, rest), (3, rest)):
+        for t, piece in ((0, first), (1, first), (0, rest), (3, first), (1, rest), (2, first), (2, rest), (3, rest)):
             coarse_product(t, *piece)
 
         out_rows = out_0.rearrange("(p t) j -> p t j", t=PACK)
@@ -212,9 +219,9 @@ def tile_picked_unet1_relu_po_kernel(
         result_codes = keep.tile([P, S], U32, name="result_codes", align_bytes=64)
         word_starts = {b: a for a, b in spans(WORD_PIECES)}
 
-        def front(a, b):
+        def front(k, a, b):
             width = b - a
-            z2 = ring.tile([P, PACK, width], F32, name="z2")
+            z2 = keep.tile([P, PACK, width], F32, name="z2_%d" % a, tag="zero_bias" if k % 2 else "z2")
             for t in range(PACK):
                 nc.vector.tensor_tensor(z2[:, t, :], h[t][:].indirect(entries(par_t, a, b)), y[t][:, a:b], ADD)
             z2_rounded = round_interleaved(z2, width, "z2_rounded")
@@ -235,9 +242,9 @@ def tile_picked_unet1_relu_po_kernel(
                 nc.sync.dma_start(out_words[:, word_starts[b] : b], result_codes[:, word_starts[b] : b].bitcast(I32))
 
         pieces = spans(FINE_PIECES)
-        banks = front(*pieces[0])
+        banks = front(0, *pieces[0])
         for k, piece in enumerate(pieces):
-            ahead = front(*pieces[k + 1]) if k + 1 < len(pieces) else None
+            ahead = front(k + 1, *pieces[k + 1]) if k + 1 < len(pieces) else None
             back(*piece, banks)
             banks = ahead
         for q in range(4):

@@ -135,7 +135,7 @@ def tile_picked_unet1_relu_po_kernel(
                 else:
                     nc.scalar.activation(y[t][:, a:b], bank[:], RELU)
 
-        late = keep.tile([P, (PACK + 1) * S], F32, name="late", tag="rounded", align_bytes=64)
+        late = keep.tile([P, (PACK + 1) * S], F32, name="late", tag="late", align_bytes=64)
         ordered_all = late[:, S:].rearrange("p (t c) -> p t c", t=PACK)
         w2_rounded = late[:, :S].bitcast(BF16).rearrange("p (t m j) -> p t m j", t=PACK, j=PACK)
         w2_halves = [load_weight_half(w2, u, "w2") for u in range(2)]
@@ -148,7 +148,7 @@ def tile_picked_unet1_relu_po_kernel(
         residual = keep.tile([P, PACK, S], F32, name="residual", tag="wide", align_bytes=64)
         nc.sync.dma_start(residual[:], res.rearrange("(p t) j -> p t j", t=PACK))
 
-        h = [keep.tile([P, V], F32, name="h%d" % t) for t in range(PACK)]
+        h = [keep.tile([P, V], F32, name="h%d" % t, align_bytes=64) for t in range(PACK)]
         for t in range(PACK - 1):
             nc.vector.tensor_copy(ordered_all[:, t, :], y[t][:].indirect(order_t[:]))
         def gather_last_plane(a, b):
@@ -182,9 +182,9 @@ def tile_picked_unet1_relu_po_kernel(
             coarse = slice(a // 2, b // 2)
             bank = psum.tile([P, (b - a) // 2], F32, name="bank")
             nc.tensor.matmul_mx(bank[:], w2_codes[:, cols].bitcast(FP8X4), w2_scales[:, cols], z_codes[:, coarse].bitcast(FP8X4), z_scales[:, coarse], start=True, stop=True)
-            if (t, a) == (PACK - 1, 0):
+            if (t, a) == (1, 0):
                 nc.vector.tensor_scalar_max(h[t][:, coarse], bank[:], 0.0)
-            elif t == PACK - 1:
+            elif (t, b) == (PACK - 1, S):
                 nc.scalar.activation(h[t][:, coarse], bank[:], RELU, bias=zero_bias[:])
             else:
                 nc.scalar.activation(h[t][:, coarse], bank[:], RELU)
@@ -201,27 +201,27 @@ def tile_picked_unet1_relu_po_kernel(
         z_second = largest_parted(*second, "z_second")
         quantise_z(z_first, *first)
         z_last = largest_parted(*last, "z_last")
-        w2_pairs.append(quantise_weight(w2_rounded[:, 2:], 2 * P, "w2_high", "z_first"))
         quantise_z(z_second, *second)
         quantise_z(z_last, *last)
-        w3_codes = keep.tile([P, N], U32, name="w3_codes", tag="z_second", align_bytes=64)
+        w2_pairs.append(quantise_weight(w2_rounded[:, 2:], 2 * P, "w2_high", "z_second"))
+        w3_codes = keep.tile([P, N], U32, name="w3_codes", tag="z_last", align_bytes=64)
         nc.vector.tensor_copy(w3_codes[:].rearrange("p (t m) -> p m t", t=PACK), w3_raw[:].rearrange("p (m t) -> p m t", t=PACK))
-        w3_planes = keep.tile([P, N], U8, name="w3_planes", tag="z_last", align_bytes=64)
+        w3_planes = keep.tile([P, N], U8, name="w3_planes", tag="late", align_bytes=64)
         nc.vector.tensor_copy(w3_planes[:].rearrange("p (t m) -> p m t", t=PACK), w3_rows[:].rearrange("p (m t) -> p m t", t=PACK))
         rest = (second[0], S)
-        for t, piece in ((0, first), (1, first), (0, rest), (3, first), (1, rest), (2, first), (2, rest), (3, rest)):
+        for t, piece in ((0, first), (1, first), (0, second), (0, last), (1, rest), (2, first), (2, rest), (3, first), (3, rest)):
             coarse_product(t, *piece)
 
         out_rows = out_0.rearrange("(p t) j -> p t j", t=PACK)
         out_words = out_1[0].rearrange("p n r -> p (n r)").bitcast(I32)
-        out_scales = keep.tile([P, S], U8, name="out_scales", align_bytes=64)
-
-        result_codes = keep.tile([P, S], U32, name="result_codes", align_bytes=64)
         word_starts = {b: a for a, b in spans(WORD_PIECES)}
+        pieces = spans(FINE_PIECES)
 
-        def front(k, a, b):
+        def front(k):
+            a, b = pieces[k]
             width = b - a
-            z2 = keep.tile([P, PACK, width], F32, name="z2_%d" % a, tag="zero_bias" if k % 2 else "z2")
+            tag = "zero_bias" if k % 2 else "z2"
+            z2 = keep.tile([P, PACK, width], F32, name="z2_%d" % a, tag=tag)
             for t in range(PACK):
                 nc.vector.tensor_tensor(z2[:, t, :], h[t][:].indirect(entries(par_t, a, b)), y[t][:, a:b], ADD)
             z2_rounded = round_interleaved(z2, width, "z2_rounded")
@@ -230,23 +230,28 @@ def tile_picked_unet1_relu_po_kernel(
             nc.vector.quantize_mx(z2_codes[:].bitcast(FP8X4), z2_scales[:], z2_rounded[:])
             return product(w3_codes, w3_planes, z2_codes[:], z2_scales[:], width, 2 if b == S else BANK // width)
 
-        def back(a, b, banks):
+        def add_residual(k, banks):
+            a, b = pieces[k]
             width = b - a
             result = ring.tile([P, PACK, width], F32, name="result", bufs=5)
             for t0, count, bank in banks:
-                nc.vector.tensor_tensor(result[:, t0 : t0 + count, :], bank[:], residual[:, t0 : t0 + count, a:b], ADD)
+                held = residual[:, t0 : t0 + count, a:b]
+                nc.vector.tensor_tensor(result[:, t0 : t0 + count, :], bank[:], held, ADD)
             nc.sync.dma_start(out_rows[:, :, a:b], result[:])
-            result_rounded = round_interleaved(result, width, "result_rounded", b == S)
+            return round_interleaved(result, width, "result_rounded", b == S)
+
+        banks = front(0)
+        rounded = []
+        for k in range(len(pieces)):
+            ahead = front(k + 1) if k + 1 < len(pieces) else None
+            rounded.append(add_residual(k, banks))
+            banks = ahead
+        out_scales = keep.tile([P, S], U8, name="out_scales", tag="h2", align_bytes=64)
+        result_codes = keep.tile([P, S], U32, name="result_codes", align_bytes=64)
+        for (a, b), result_rounded in zip(pieces, rounded):
             nc.vector.quantize_mx(result_codes[:, a:b].bitcast(FP8X4), out_scales[:, a:b], result_rounded[:])
             if b in word_starts:
                 nc.sync.dma_start(out_words[:, word_starts[b] : b], result_codes[:, word_starts[b] : b].bitcast(I32))
-
-        pieces = spans(FINE_PIECES)
-        banks = front(0, *pieces[0])
-        for k, piece in enumerate(pieces):
-            ahead = front(k + 1, *pieces[k + 1]) if k + 1 < len(pieces) else None
-            back(*piece, banks)
-            banks = ahead
         for q in range(4):
             queue = nc.sync if q < 2 else nc.scalar
             queue.dma_start(out_2[0, 4 * q : 4 * q + 4, :].bitcast(I32), out_scales[32 * q : 32 * q + 4, :].bitcast(I32))

@@ -22,6 +22,7 @@ PACK = 4
 LANES = 16
 BANK = 512
 LAST_PLANE_PIECES = (256, 256, 256, 256)
+FIRST_PLANE_BANKS = (256, 256, 256, 128, 128)
 PICK_PIECES = (512, 256, 256)
 POOL_PIECES = (512, 256, 256)
 FINE_PIECES = (256, 256, 256, 128, 128)
@@ -57,15 +58,15 @@ def tile_picked_unet1_relu_po_kernel(
                 queue.dma_start(plane[32 * q : 32 * q + 4, :].bitcast(I32), source[0, 4 * q : 4 * q + 4, :].bitcast(I32))
             return plane
 
-        def load_weight_half(w, u, name):
-            raw = keep.tile([P, PACK, H // 2], F32, name="%s_raw%d" % (name, u), tag="weight_raw%d" % u)
+        def load_weight_half(w, u, name, tag):
+            raw = keep.tile([P, PACK, H // 2], F32, name="%s_raw%d" % (name, u), tag=tag)
             nc.sync.dma_start(raw[:], w.rearrange("(p j) c -> p j c", j=PACK)[:, :, u * H // 2 : (u + 1) * H // 2])
             return raw
 
-        def round_weight_half(raw, u, rounded):
+        def round_weight_rows(raw, start, a, b, rounded):
             nc.scalar.activation(
-                rounded[:, :, u * P // 2 : (u + 1) * P // 2, :].rearrange("p t m j -> p m j t"),
-                raw[:].rearrange("p j (m t) -> p m j t", t=PACK),
+                rounded[:, :, start + a : start + b, :].rearrange("p t m j -> p m j t"),
+                raw[:].rearrange("p j (m t) -> p m j t", t=PACK)[:, a:b],
                 COPY,
             )
 
@@ -95,12 +96,13 @@ def tile_picked_unet1_relu_po_kernel(
                 nc.scalar.activation(target, source, COPY)
             return rounded
 
-        w1_low = load_weight_half(w1, 0, "w1")
+        w1_low = load_weight_half(w1, 0, "w1", "raw_low")
         offs_t = load_list(offs, "offs_t")
         x_rows = load_scale_rows(x_scales, T, "x_rows", nc.sync)
         x_table = keep.tile([P, T], U32, name="x_table", tag="wide", align_bytes=64)
         nc.sync.dma_start(x_table[:].bitcast(I32), x_words[0].rearrange("p n r -> p (n r)").bitcast(I32))
-        w1_high = load_weight_half(w1, 1, "w1")
+        w1_high = load_weight_half(w1, 1, "w1", "raw_high")
+        w2_low = load_weight_half(w2, 0, "w2", "w2_raw_low")
         order_t = load_list(order, "order_t")
         par_t = load_list(par, "par_t")
 
@@ -127,10 +129,13 @@ def tile_picked_unet1_relu_po_kernel(
         y = [keep.tile([P, S if t == PACK - 1 else 2 * S], F32, name="y%d" % t) for t in range(PACK)]
         for t, (w1_codes, w1_scales, start) in enumerate(w1_planes):
             cols = slice(start, start + P)
-            for i, (words, (a, b)) in enumerate(zip(picked, spans(PICK_PIECES))):
+            for a, b in spans(FIRST_PLANE_BANKS if t == 0 else (BANK, BANK)):
                 bank = psum.tile([P, b - a], F32, name="bank")
-                nc.tensor.matmul_mx(bank[:], w1_codes[:, cols].bitcast(FP8X4), w1_scales[:, cols], words[:].bitcast(FP8X4), picked_scales[:, a:b], start=True, stop=True)
-                if t == 0 and i == 1:
+                for words, (c, d) in zip(picked, spans(PICK_PIECES)):
+                    lo, hi = max(a, c), min(b, d)
+                    if lo < hi:
+                        nc.tensor.matmul_mx(bank[:, lo - a : hi - a], w1_codes[:, cols].bitcast(FP8X4), w1_scales[:, cols], words[:, lo - c : hi - c].bitcast(FP8X4), picked_scales[:, lo:hi], start=True, stop=True)
+                if t == 0 and a == PICK_PIECES[0]:
                     nc.vector.tensor_scalar_max(y[t][:, a:b], bank[:], 0.0)
                 else:
                     nc.scalar.activation(y[t][:, a:b], bank[:], RELU)
@@ -138,11 +143,12 @@ def tile_picked_unet1_relu_po_kernel(
         late = keep.tile([P, (PACK + 1) * S], F32, name="late", tag="late", align_bytes=64)
         ordered_all = late[:, S:].rearrange("p (t c) -> p t c", t=PACK)
         w2_rounded = late[:, :S].bitcast(BF16).rearrange("p (t m j) -> p t m j", t=PACK, j=PACK)
-        w2_halves = [load_weight_half(w2, u, "w2") for u in range(2)]
-        for u, raw in enumerate(w2_halves):
-            round_weight_half(raw, u, w2_rounded)
+        w2_high = load_weight_half(w2, 1, "w2", "raw_low")
+        round_weight_rows(w2_low, 0, 0, P // 4, w2_rounded)
+        round_weight_rows(w2_low, 0, P // 4, P // 2, w2_rounded)
+        round_weight_rows(w2_high, P // 2, 0, P // 2, w2_rounded)
         w2_pairs = [quantise_weight(w2_rounded[:, :2], 2 * P, "w2_low", "w2_low")]
-        w3_raw = keep.tile([P, N], U32, name="w3_raw", tag="weight_raw0")
+        w3_raw = keep.tile([P, N], U32, name="w3_raw", tag="raw_high")
         nc.sync.dma_start(w3_raw[:].bitcast(I32), w3_words[0].rearrange("p n r -> p (n r)").bitcast(I32))
         w3_rows = load_scale_rows(w3_scales, N, "w3_rows", nc.sync)
         residual = keep.tile([P, PACK, S], F32, name="residual", tag="wide", align_bytes=64)

@@ -58,9 +58,10 @@ def tile_picked_unet1_relu_po_kernel(
                 queue.dma_start(plane[32 * q : 32 * q + 4, :].bitcast(I32), source[0, 4 * q : 4 * q + 4, :].bitcast(I32))
             return plane
 
-        def load_weight_half(w, u, name, tag):
+        def load_weight_half(w, u, name, tag, parts=(H // 2,)):
             raw = keep.tile([P, PACK, H // 2], F32, name="%s_raw%d" % (name, u), tag=tag)
-            nc.sync.dma_start(raw[:], w.rearrange("(p j) c -> p j c", j=PACK)[:, :, u * H // 2 : (u + 1) * H // 2])
+            for a, b in spans(parts):
+                nc.sync.dma_start(raw[:, :, a:b], w.rearrange("(p j) c -> p j c", j=PACK)[:, :, u * H // 2 + a : u * H // 2 + b])
             return raw
 
         def round_weight_rows(raw, start, a, b, rounded):
@@ -101,7 +102,7 @@ def tile_picked_unet1_relu_po_kernel(
         x_rows = load_scale_rows(x_scales, T, "x_rows", nc.sync)
         x_table = keep.tile([P, T], U32, name="x_table", tag="wide", align_bytes=64)
         nc.sync.dma_start(x_table[:].bitcast(I32), x_words[0].rearrange("p n r -> p (n r)").bitcast(I32))
-        w1_high = load_weight_half(w1, 1, "w1", "raw_high")
+        w1_high = load_weight_half(w1, 1, "w1", "raw_high", (H // 4, H // 4))
         w2_low = load_weight_half(w2, 0, "w2", "w2_raw_low")
         order_t = load_list(order, "order_t")
         par_t = load_list(par, "par_t")
@@ -111,10 +112,11 @@ def tile_picked_unet1_relu_po_kernel(
         first_rounded = keep.tile([P, 1, P, PACK], BF16, name="first_rounded", align_bytes=64)
         other_rounded = keep.tile([P, PACK - 1, P, PACK], BF16, name="other_rounded", tag="rounded", align_bytes=64)
         for u, raw in enumerate((w1_low, w1_high)):
-            source = raw[:].rearrange("p j (m t) -> p m t j", t=PACK)
-            rows = slice(u * P // 2, (u + 1) * P // 2)
-            nc.scalar.activation(first_rounded[:, :, rows, :].rearrange("p t m j -> p m t j"), source[:, :, :1, :], COPY)
-            nc.scalar.activation(other_rounded[:, :, rows, :].rearrange("p t m j -> p m t j"), source[:, :, 1:, :], COPY)
+            source = raw[:].rearrange("p j (m t) -> p m j t", t=PACK)
+            start = u * P // 2
+            for a, b in spans((P // 4, P // 4) if u else (P // 2,)):
+                nc.scalar.activation(first_rounded[:, :, start + a : start + b, :].rearrange("p t m j -> p m j t"), source[:, a:b, :, :1], COPY)
+            nc.scalar.activation(other_rounded[:, :, start : start + P // 2, :].rearrange("p t m j -> p m j t"), source[:, :, :, 1:], COPY)
         w1_planes = [quantise_weight(first_rounded[:], P, "w1_first", "w1_first") + (0,)]
         picked = []
         for a, b in spans(PICK_PIECES):

@@ -23,10 +23,11 @@ LANES = 16
 BANK = 512
 LAST_PLANE_PIECES = (256, 256, 256, 256)
 FIRST_PLANE_BANKS = (256, 256, 256, 128, 128)
+W1_LOADS = (192, 192, 128)
 PICK_PIECES = (512, 256, 256)
 POOL_PIECES = (512, 256, 256)
 FINE_PIECES = (256, 256, 256, 128, 128)
-WORD_PIECES = (512, 384, 128)
+WORD_PIECES = (512, 256, 256)
 
 
 def spans(widths):
@@ -58,10 +59,10 @@ def tile_picked_unet1_relu_po_kernel(
                 queue.dma_start(plane[32 * q : 32 * q + 4, :].bitcast(I32), source[0, 4 * q : 4 * q + 4, :].bitcast(I32))
             return plane
 
-        def load_weight_half(w, u, name, tag, parts=(H // 2,)):
-            raw = keep.tile([P, PACK, H // 2], F32, name="%s_raw%d" % (name, u), tag=tag)
+        def load_weight_columns(w, start, parts, name, tag):
+            raw = keep.tile([P, PACK, sum(parts)], F32, name=name, tag=tag)
             for a, b in spans(parts):
-                nc.sync.dma_start(raw[:, :, a:b], w.rearrange("(p j) c -> p j c", j=PACK)[:, :, u * H // 2 + a : u * H // 2 + b])
+                nc.sync.dma_start(raw[:, :, a:b], w.rearrange("(p j) c -> p j c", j=PACK)[:, :, start + a : start + b])
             return raw
 
         def round_weight_rows(raw, start, a, b, rounded):
@@ -97,13 +98,13 @@ def tile_picked_unet1_relu_po_kernel(
                 nc.scalar.activation(target, source, COPY)
             return rounded
 
-        w1_low = load_weight_half(w1, 0, "w1", "raw_low")
+        w1_low = load_weight_columns(w1, 0, W1_LOADS[:1], "w1_low", "raw_low")
         offs_t = load_list(offs, "offs_t")
         x_rows = load_scale_rows(x_scales, T, "x_rows", nc.sync)
         x_table = keep.tile([P, T], U32, name="x_table", tag="wide", align_bytes=64)
         nc.sync.dma_start(x_table[:].bitcast(I32), x_words[0].rearrange("p n r -> p (n r)").bitcast(I32))
-        w1_high = load_weight_half(w1, 1, "w1", "raw_high", (H // 4, H // 4))
-        w2_low = load_weight_half(w2, 0, "w2", "w2_raw_low")
+        w1_high = load_weight_columns(w1, W1_LOADS[0], W1_LOADS[1:], "w1_high", "raw_high")
+        w2_low = load_weight_columns(w2, 0, (H // 2,), "w2_low", "w2_raw_low")
         order_t = load_list(order, "order_t")
         par_t = load_list(par, "par_t")
 
@@ -111,12 +112,11 @@ def tile_picked_unet1_relu_po_kernel(
         nc.vector.tensor_copy(picked_scales[:], x_rows[:].indirect(offs_t[:]))
         first_rounded = keep.tile([P, 1, P, PACK], BF16, name="first_rounded", align_bytes=64)
         other_rounded = keep.tile([P, PACK - 1, P, PACK], BF16, name="other_rounded", tag="rounded", align_bytes=64)
-        for u, raw in enumerate((w1_low, w1_high)):
+        for raw, start, parts in ((w1_low, 0, W1_LOADS[:1]), (w1_high, W1_LOADS[0] // PACK, W1_LOADS[1:])):
             source = raw[:].rearrange("p j (m t) -> p m j t", t=PACK)
-            start = u * P // 2
-            for a, b in spans((P // 4, P // 4) if u else (P // 2,)):
+            for a, b in spans([part // PACK for part in parts]):
                 nc.scalar.activation(first_rounded[:, :, start + a : start + b, :].rearrange("p t m j -> p m j t"), source[:, a:b, :, :1], COPY)
-            nc.scalar.activation(other_rounded[:, :, start : start + P // 2, :].rearrange("p t m j -> p m j t"), source[:, :, :, 1:], COPY)
+            nc.scalar.activation(other_rounded[:, :, start : start + sum(parts) // PACK, :].rearrange("p t m j -> p m j t"), source[:, :, :, 1:], COPY)
         w1_planes = [quantise_weight(first_rounded[:], P, "w1_first", "w1_first") + (0,)]
         picked = []
         for a, b in spans(PICK_PIECES):
@@ -137,7 +137,7 @@ def tile_picked_unet1_relu_po_kernel(
                     lo, hi = max(a, c), min(b, d)
                     if lo < hi:
                         nc.tensor.matmul_mx(bank[:, lo - a : hi - a], w1_codes[:, cols].bitcast(FP8X4), w1_scales[:, cols], words[:, lo - c : hi - c].bitcast(FP8X4), picked_scales[:, lo:hi], start=True, stop=True)
-                if t == 0 and a == PICK_PIECES[0]:
+                if t == 0 and a in (0, PICK_PIECES[0]):
                     nc.vector.tensor_scalar_max(y[t][:, a:b], bank[:], 0.0)
                 else:
                     nc.scalar.activation(y[t][:, a:b], bank[:], RELU)
@@ -145,7 +145,7 @@ def tile_picked_unet1_relu_po_kernel(
         late = keep.tile([P, (PACK + 1) * S], F32, name="late", tag="late", align_bytes=64)
         ordered_all = late[:, S:].rearrange("p (t c) -> p t c", t=PACK)
         w2_rounded = late[:, :S].bitcast(BF16).rearrange("p (t m j) -> p t m j", t=PACK, j=PACK)
-        w2_high = load_weight_half(w2, 1, "w2", "raw_low")
+        w2_high = load_weight_columns(w2, H // 2, (H // 2,), "w2_high", "raw_low")
         round_weight_rows(w2_low, 0, 0, P // 4, w2_rounded)
         round_weight_rows(w2_low, 0, P // 4, P // 2, w2_rounded)
         round_weight_rows(w2_high, P // 2, 0, P // 2, w2_rounded)
@@ -245,7 +245,10 @@ def tile_picked_unet1_relu_po_kernel(
             for t0, count, bank in banks:
                 held = residual[:, t0 : t0 + count, a:b]
                 nc.vector.tensor_tensor(result[:, t0 : t0 + count, :], bank[:], held, ADD)
-            nc.sync.dma_start(out_rows[:, :, a:b], result[:])
+                if k == 2:
+                    nc.sync.dma_start(out_rows[:, t0 : t0 + count, a:b], result[:, t0 : t0 + count, :])
+            if k != 2:
+                nc.sync.dma_start(out_rows[:, :, a:b], result[:])
             return round_interleaved(result, width, "result_rounded", b == S)
 
         banks = front(0)

@@ -176,8 +176,6 @@ def tile_picked_unet1_relu_po_kernel(
             nc.vector.tensor_tensor(z[:].rearrange("p (c u s) -> p c u s", u=2, s=2), sides[0], sides[1], MAX)
             return z
 
-        zero_bias = keep.tile([P, 1], F32, name="zero_bias")
-        nc.vector.memset(zero_bias[:], 0.0)
         z_codes = keep.tile([P, V], U32, name="z_codes", align_bytes=64)
         z_scales = keep.tile([P, V], U8, name="z_scales", align_bytes=64)
 
@@ -192,8 +190,6 @@ def tile_picked_unet1_relu_po_kernel(
             nc.tensor.matmul_mx(bank[:], w2_codes[:, cols].bitcast(FP8X4), w2_scales[:, cols], z_codes[:, coarse].bitcast(FP8X4), z_scales[:, coarse], start=True, stop=True)
             if (t, a) == (1, 0):
                 nc.vector.tensor_scalar_max(h[t][:, coarse], bank[:], 0.0)
-            elif (t, b) == (PACK - 1, S):
-                nc.scalar.activation(h[t][:, coarse], bank[:], RELU, bias=zero_bias[:])
             else:
                 nc.scalar.activation(h[t][:, coarse], bank[:], RELU)
 
@@ -228,8 +224,8 @@ def tile_picked_unet1_relu_po_kernel(
         def front(k):
             a, b = pieces[k]
             width = b - a
-            tag = "zero_bias" if k % 2 else "z2"
-            z2 = keep.tile([P, PACK, width], F32, name="z2_%d" % a, tag=tag)
+            tag = "z_codes" if k % 2 else "z2"
+            z2 = keep.tile([P, PACK, width], F32, name="z2_%d" % a, tag=tag, align_bytes=64)
             for t in range(PACK):
                 nc.vector.tensor_tensor(z2[:, t, :], h[t][:].indirect(entries(par_t, a, b)), y[t][:, a:b], ADD)
             z2_rounded = round_interleaved(z2, width, "z2_rounded")

@@ -21,12 +21,16 @@ P = 128
 PACK = 4
 LANES = 16
 BANK = 512
-LAST_PLANE_PIECES = (256, 256, 256, 256)
-FIRST_PLANE_BANKS = (256, 256, 256, 128, 128)
+LINE = 4
+QUADRANTS = 4
+
 W1_LOADS = (192, 192, 128)
 PICK_PIECES = (512, 256, 256)
+FIRST_PLANE_BANKS = (256, 256, 256, 128, 128)
+LAST_PLANE_PIECES = (256, 256, 256, 256)
 POOL_PIECES = (512, 256, 256)
 FINE_PIECES = (256, 256, 256, 128, 128)
+STORED_BY_BANK = 2
 WORD_PIECES = (512, 256, 256)
 
 
@@ -52,12 +56,12 @@ def tile_picked_unet1_relu_po_kernel(
         def entries(held, a, b):
             return held[:, a // LANES : b // LANES]
 
-        def load_scale_rows(source, width, name, queue):
-            plane = keep.tile([P, width], U8, name=name, align_bytes=64)
-            nc.vector.memset(plane[:].bitcast(I32), 0)
-            for q in range(4):
-                queue.dma_start(plane[32 * q : 32 * q + 4, :].bitcast(I32), source[0, 4 * q : 4 * q + 4, :].bitcast(I32))
-            return plane
+        def load_scale_rows(source, width, name):
+            rows = keep.tile([P, width], U8, name=name, align_bytes=64)
+            nc.vector.memset(rows[:].bitcast(I32), 0)
+            for q in range(QUADRANTS):
+                nc.sync.dma_start(rows[32 * q : 32 * q + 4, :].bitcast(I32), source[0, 4 * q : 4 * q + 4, :].bitcast(I32))
+            return rows
 
         def load_weight_columns(w, start, parts, name, tag):
             raw = keep.tile([P, PACK, sum(parts)], F32, name=name, tag=tag)
@@ -65,12 +69,11 @@ def tile_picked_unet1_relu_po_kernel(
                 nc.sync.dma_start(raw[:, :, a:b], w.rearrange("(p j) c -> p j c", j=PACK)[:, :, start + a : start + b])
             return raw
 
-        def round_weight_rows(raw, start, a, b, rounded):
-            nc.scalar.activation(
-                rounded[:, :, start + a : start + b, :].rearrange("p t m j -> p m j t"),
-                raw[:].rearrange("p j (m t) -> p m j t", t=PACK)[:, a:b],
-                COPY,
-            )
+        def dealt(rounded):
+            return rounded.rearrange("p t m j -> p m j t")
+
+        def by_lines(raw):
+            return raw[:].rearrange("p j (m t) -> p m j t", t=PACK)
 
         def quantise_weight(rounded, width, name, tag):
             codes = keep.tile([P, width], U32, name=name + "_codes", tag=tag, align_bytes=64)
@@ -78,20 +81,16 @@ def tile_picked_unet1_relu_po_kernel(
             nc.vector.quantize_mx(codes[:].bitcast(FP8X4), scales[:], rounded.rearrange("p t m j -> p (t m j)"))
             return codes, scales
 
-        def product(w_codes, w_scales, codes, scales, width, per_bank):
-            banks = []
-            for t0 in range(0, PACK, per_bank):
-                bank = psum.tile([P, per_bank, width], F32, name="bank")
-                for i in range(per_bank):
-                    cols = slice((t0 + i) * P, (t0 + i + 1) * P)
-                    nc.tensor.matmul_mx(bank[:, i, :], w_codes[:, cols].bitcast(FP8X4), w_scales[:, cols], codes.bitcast(FP8X4), scales, start=True, stop=True)
-                banks.append((t0, per_bank, bank))
-            return banks
+        def relu(out, bank, on_vector):
+            if on_vector:
+                nc.vector.tensor_scalar_max(out, bank, 0.0)
+            else:
+                nc.scalar.activation(out, bank, RELU)
 
-        def round_interleaved(values, width, name, on_vector=False):
-            rounded = ring.tile([P, width * PACK], BF16, name=name, align_bytes=64, bufs=5 if name == "result_rounded" else 2)
-            target = rounded[:].rearrange("p (c i t) -> p c t i", i=4, t=PACK)
-            source = values[:].rearrange("p t (c i) -> p c t i", i=4)
+        def round_interleaved(values, width, name, bufs, on_vector):
+            rounded = ring.tile([P, width * PACK], BF16, name=name, align_bytes=64, bufs=bufs)
+            target = rounded[:].rearrange("p (c i t) -> p c t i", i=LINE, t=PACK)
+            source = values[:].rearrange("p t (c i) -> p c t i", i=LINE)
             if on_vector:
                 nc.vector.tensor_copy(target, source)
             else:
@@ -100,7 +99,7 @@ def tile_picked_unet1_relu_po_kernel(
 
         w1_low = load_weight_columns(w1, 0, W1_LOADS[:1], "w1_low", "raw_low")
         offs_t = load_list(offs, "offs_t")
-        x_rows = load_scale_rows(x_scales, T, "x_rows", nc.sync)
+        x_rows = load_scale_rows(x_scales, T, "x_rows")
         x_table = keep.tile([P, T], U32, name="x_table", tag="wide", align_bytes=64)
         nc.sync.dma_start(x_table[:].bitcast(I32), x_words[0].rearrange("p n r -> p (n r)").bitcast(I32))
         w1_high = load_weight_columns(w1, W1_LOADS[0], W1_LOADS[1:], "w1_high", "raw_high")
@@ -113,10 +112,9 @@ def tile_picked_unet1_relu_po_kernel(
         first_rounded = keep.tile([P, 1, P, PACK], BF16, name="first_rounded", align_bytes=64)
         other_rounded = keep.tile([P, PACK - 1, P, PACK], BF16, name="other_rounded", tag="rounded", align_bytes=64)
         for raw, start, parts in ((w1_low, 0, W1_LOADS[:1]), (w1_high, W1_LOADS[0] // PACK, W1_LOADS[1:])):
-            source = raw[:].rearrange("p j (m t) -> p m j t", t=PACK)
             for a, b in spans([part // PACK for part in parts]):
-                nc.scalar.activation(first_rounded[:, :, start + a : start + b, :].rearrange("p t m j -> p m j t"), source[:, a:b, :, :1], COPY)
-            nc.scalar.activation(other_rounded[:, :, start : start + sum(parts) // PACK, :].rearrange("p t m j -> p m j t"), source[:, :, :, 1:], COPY)
+                nc.scalar.activation(dealt(first_rounded[:, :, start + a : start + b, :]), by_lines(raw)[:, a:b, :, :1], COPY)
+            nc.scalar.activation(dealt(other_rounded[:, :, start : start + sum(parts) // PACK, :]), by_lines(raw)[:, :, :, 1:], COPY)
         w1_planes = [quantise_weight(first_rounded[:], P, "w1_first", "w1_first") + (0,)]
         picked = []
         for a, b in spans(PICK_PIECES):
@@ -131,49 +129,54 @@ def tile_picked_unet1_relu_po_kernel(
         y = [keep.tile([P, S if t == PACK - 1 else 2 * S], F32, name="y%d" % t) for t in range(PACK)]
         for t, (w1_codes, w1_scales, start) in enumerate(w1_planes):
             cols = slice(start, start + P)
-            for a, b in spans(FIRST_PLANE_BANKS if t == 0 else (BANK, BANK)):
+            for n, (a, b) in enumerate(spans(FIRST_PLANE_BANKS if t == 0 else (BANK, BANK))):
                 bank = psum.tile([P, b - a], F32, name="bank")
                 for words, (c, d) in zip(picked, spans(PICK_PIECES)):
                     lo, hi = max(a, c), min(b, d)
                     if lo < hi:
-                        nc.tensor.matmul_mx(bank[:, lo - a : hi - a], w1_codes[:, cols].bitcast(FP8X4), w1_scales[:, cols], words[:, lo - c : hi - c].bitcast(FP8X4), picked_scales[:, lo:hi], start=True, stop=True)
-                if t == 0 and a in (0, PICK_PIECES[0]):
-                    nc.vector.tensor_scalar_max(y[t][:, a:b], bank[:], 0.0)
-                else:
-                    nc.scalar.activation(y[t][:, a:b], bank[:], RELU)
+                        nc.tensor.matmul_mx(
+                            bank[:, lo - a : hi - a],
+                            w1_codes[:, cols].bitcast(FP8X4),
+                            w1_scales[:, cols],
+                            words[:, lo - c : hi - c].bitcast(FP8X4),
+                            picked_scales[:, lo:hi],
+                            start=True,
+                            stop=True,
+                        )
+                relu(y[t][:, a:b], bank[:], t == 0 and n in (0, 2))
 
         late = keep.tile([P, (PACK + 1) * S], F32, name="late", tag="late", align_bytes=64)
-        ordered_all = late[:, S:].rearrange("p (t c) -> p t c", t=PACK)
+        ordered = late[:, S:].rearrange("p (t c) -> p t c", t=PACK)
         w2_rounded = late[:, :S].bitcast(BF16).rearrange("p (t m j) -> p t m j", t=PACK, j=PACK)
         w2_high = load_weight_columns(w2, H // 2, (H // 2,), "w2_high", "raw_low")
-        round_weight_rows(w2_low, 0, 0, P // 4, w2_rounded)
-        round_weight_rows(w2_low, 0, P // 4, P // 2, w2_rounded)
-        round_weight_rows(w2_high, P // 2, 0, P // 2, w2_rounded)
+        for raw, start, a, b in ((w2_low, 0, 0, P // 4), (w2_low, 0, P // 4, P // 2), (w2_high, P // 2, 0, P // 2)):
+            nc.scalar.activation(dealt(w2_rounded[:, :, start + a : start + b, :]), by_lines(raw)[:, a:b], COPY)
         w2_pairs = [quantise_weight(w2_rounded[:, :2], 2 * P, "w2_low", "w2_low")]
+
         w3_raw = keep.tile([P, N], U32, name="w3_raw", tag="raw_high")
         nc.sync.dma_start(w3_raw[:].bitcast(I32), w3_words[0].rearrange("p n r -> p (n r)").bitcast(I32))
-        w3_rows = load_scale_rows(w3_scales, N, "w3_rows", nc.sync)
+        w3_rows = load_scale_rows(w3_scales, N, "w3_rows")
         residual = keep.tile([P, PACK, S], F32, name="residual", tag="wide", align_bytes=64)
         nc.sync.dma_start(residual[:], res.rearrange("(p t) j -> p t j", t=PACK))
 
         h = [keep.tile([P, V], F32, name="h%d" % t, align_bytes=64) for t in range(PACK)]
         for t in range(PACK - 1):
-            nc.vector.tensor_copy(ordered_all[:, t, :], y[t][:].indirect(order_t[:]))
-        def gather_last_plane(a, b):
-            nc.vector.tensor_copy(ordered_all[:, PACK - 1, a:b], y[PACK - 1][:].indirect(entries(order_t, a, b)))
+            nc.vector.tensor_copy(ordered[:, t, :], y[t][:].indirect(order_t[:]))
+
+        parted = {}
 
         def part_pairs(u, a, b):
-            start = max(first for first in parted if first <= a)
+            start = max(begin for begin in parted if begin <= a)
             target = parted[start][:, :, u, (a - start) // 2 : (b - start) // 2, :]
             nc.scalar.copy(
-                target.rearrange("p e (c i) s -> p c s i e", i=4),
-                ordered_all[:, 2 * u : 2 * u + 2, a:b].rearrange("p s (c i e) -> p c s i e", i=4, e=2),
+                target.rearrange("p e (c i) s -> p c s i e", i=LINE),
+                ordered[:, 2 * u : 2 * u + 2, a:b].rearrange("p s (c i e) -> p c s i e", i=LINE, e=2),
             )
 
-        def largest_parted(a, b, name):
+        def largest(a, b, name):
             z = keep.tile([P, (b - a) // 2 * PACK], BF16, name=name, align_bytes=64)
-            sides = [parted[a][:, e].rearrange("p u c s -> p c u s") for e in range(2)]
-            nc.vector.tensor_tensor(z[:].rearrange("p (c u s) -> p c u s", u=2, s=2), sides[0], sides[1], MAX)
+            members = [parted[a][:, e].rearrange("p u c s -> p c u s") for e in range(2)]
+            nc.vector.tensor_tensor(z[:].rearrange("p (c u s) -> p c u s", u=2, s=2), members[0], members[1], MAX)
             return z
 
         z_codes = keep.tile([P, V], U32, name="z_codes", align_bytes=64)
@@ -182,83 +185,116 @@ def tile_picked_unet1_relu_po_kernel(
         def quantise_z(z, a, b):
             nc.vector.quantize_mx(z_codes[:, a // 2 : b // 2].bitcast(FP8X4), z_scales[:, a // 2 : b // 2], z[:])
 
-        def coarse_product(t, a, b):
+        def coarse_product(t, a, b, on_vector=False):
             w2_codes, w2_scales = w2_pairs[t // 2]
             cols = slice(t % 2 * P, (t % 2 + 1) * P)
             coarse = slice(a // 2, b // 2)
             bank = psum.tile([P, (b - a) // 2], F32, name="bank")
-            nc.tensor.matmul_mx(bank[:], w2_codes[:, cols].bitcast(FP8X4), w2_scales[:, cols], z_codes[:, coarse].bitcast(FP8X4), z_scales[:, coarse], start=True, stop=True)
-            if (t, a) == (1, 0):
-                nc.vector.tensor_scalar_max(h[t][:, coarse], bank[:], 0.0)
-            else:
-                nc.scalar.activation(h[t][:, coarse], bank[:], RELU)
+            nc.tensor.matmul_mx(
+                bank[:],
+                w2_codes[:, cols].bitcast(FP8X4),
+                w2_scales[:, cols],
+                z_codes[:, coarse].bitcast(FP8X4),
+                z_scales[:, coarse],
+                start=True,
+                stop=True,
+            )
+            relu(h[t][:, coarse], bank[:], on_vector)
 
         first, second, last = spans(POOL_PIECES)
-        parted = {}
         for (a, b), tag in zip((first, second, last), ("first_rounded", "picked_scales", "w1_last")):
             parted[a] = keep.tile([P, 2, 2, (b - a) // 2, 2], BF16, name="parted%d" % a, tag=tag, align_bytes=64)
             part_pairs(0, a, b)
-        for piece in spans(LAST_PLANE_PIECES):
-            gather_last_plane(*piece)
-            part_pairs(1, *piece)
-        z_first = largest_parted(*first, "z_first")
-        z_second = largest_parted(*second, "z_second")
+        for a, b in spans(LAST_PLANE_PIECES):
+            nc.vector.tensor_copy(ordered[:, PACK - 1, a:b], y[PACK - 1][:].indirect(entries(order_t, a, b)))
+            part_pairs(1, a, b)
+        z_first = largest(*first, "z_first")
+        z_second = largest(*second, "z_second")
         quantise_z(z_first, *first)
-        z_last = largest_parted(*last, "z_last")
+        z_last = largest(*last, "z_last")
         quantise_z(z_second, *second)
         quantise_z(z_last, *last)
+
         w2_pairs.append(quantise_weight(w2_rounded[:, 2:], 2 * P, "w2_high", "z_second"))
         w3_codes = keep.tile([P, N], U32, name="w3_codes", tag="z_last", align_bytes=64)
         nc.vector.tensor_copy(w3_codes[:].rearrange("p (t m) -> p m t", t=PACK), w3_raw[:].rearrange("p (m t) -> p m t", t=PACK))
         w3_planes = keep.tile([P, N], U8, name="w3_planes", tag="late", align_bytes=64)
         nc.vector.tensor_copy(w3_planes[:].rearrange("p (t m) -> p m t", t=PACK), w3_rows[:].rearrange("p (m t) -> p m t", t=PACK))
-        rest = (second[0], S)
-        for t, piece in ((0, first), (1, first), (0, second), (0, last), (1, rest), (2, first), (2, rest), (3, first), (3, rest)):
-            coarse_product(t, *piece)
+
+        coarse_product(0, *first)
+        coarse_product(1, *first, on_vector=True)
+        coarse_product(0, *second)
+        coarse_product(0, *last)
+        coarse_product(1, second[0], S)
+        for t in range(2, PACK):
+            coarse_product(t, 0, S)
 
         out_rows = out_0.rearrange("(p t) j -> p t j", t=PACK)
         out_words = out_1[0].rearrange("p n r -> p (n r)").bitcast(I32)
         word_starts = {b: a for a, b in spans(WORD_PIECES)}
         pieces = spans(FINE_PIECES)
+        z2_of = {}
 
-        def front(k):
+        def gather_coarse(k, t):
+            a, b = pieces[k]
+            if t == 0:
+                z2_of[k] = ring.tile([P, PACK, b - a], F32, name="z2", align_bytes=64)
+            nc.vector.tensor_tensor(z2_of[k][:, t, :], h[t][:].indirect(entries(par_t, a, b)), y[t][:, a:b], ADD)
+
+        def fine_product(k):
             a, b = pieces[k]
             width = b - a
-            tag = "z_codes" if k % 2 else "z2"
-            z2 = keep.tile([P, PACK, width], F32, name="z2_%d" % a, tag=tag, align_bytes=64)
             for t in range(PACK):
-                nc.vector.tensor_tensor(z2[:, t, :], h[t][:].indirect(entries(par_t, a, b)), y[t][:, a:b], ADD)
-            z2_rounded = round_interleaved(z2, width, "z2_rounded")
+                if (k, t) != (1, 0):
+                    gather_coarse(k, t)
+                if (k, t) == (0, 0):
+                    gather_coarse(1, 0)
+            z2_rounded = round_interleaved(z2_of[k], width, "z2_rounded", 2, False)
             z2_codes = ring.tile([P, width], U32, name="z2_codes", align_bytes=64)
             z2_scales = ring.tile([P, width], U8, name="z2_scales", align_bytes=64)
             nc.vector.quantize_mx(z2_codes[:].bitcast(FP8X4), z2_scales[:], z2_rounded[:])
-            return product(w3_codes, w3_planes, z2_codes[:], z2_scales[:], width, 2 if b == S else BANK // width)
+            per_bank = 2 if b == S else BANK // width
+            banks = []
+            for t0 in range(0, PACK, per_bank):
+                bank = psum.tile([P, per_bank, width], F32, name="bank")
+                for i in range(per_bank):
+                    cols = slice((t0 + i) * P, (t0 + i + 1) * P)
+                    nc.tensor.matmul_mx(
+                        bank[:, i, :],
+                        w3_codes[:, cols].bitcast(FP8X4),
+                        w3_planes[:, cols],
+                        z2_codes[:].bitcast(FP8X4),
+                        z2_scales[:],
+                        start=True,
+                        stop=True,
+                    )
+                banks.append((slice(t0, t0 + per_bank), bank))
+            return banks
 
         def add_residual(k, banks):
             a, b = pieces[k]
-            width = b - a
-            result = ring.tile([P, PACK, width], F32, name="result", bufs=5)
-            for t0, count, bank in banks:
-                held = residual[:, t0 : t0 + count, a:b]
-                nc.vector.tensor_tensor(result[:, t0 : t0 + count, :], bank[:], held, ADD)
-                if k == 2:
-                    nc.sync.dma_start(out_rows[:, t0 : t0 + count, a:b], result[:, t0 : t0 + count, :])
-            if k != 2:
+            result = ring.tile([P, PACK, b - a], F32, name="result", bufs=len(pieces))
+            for planes, bank in banks:
+                nc.vector.tensor_tensor(result[:, planes, :], bank[:], residual[:, planes, a:b], ADD)
+                if k == STORED_BY_BANK:
+                    nc.sync.dma_start(out_rows[:, planes, a:b], result[:, planes, :])
+            if k != STORED_BY_BANK:
                 nc.sync.dma_start(out_rows[:, :, a:b], result[:])
-            return round_interleaved(result, width, "result_rounded", b == S)
+            return round_interleaved(result, b - a, "result_rounded", len(pieces), b == S)
 
-        banks = front(0)
-        rounded = []
+        banks = fine_product(0)
+        rounded_results = []
         for k in range(len(pieces)):
-            ahead = front(k + 1) if k + 1 < len(pieces) else None
-            rounded.append(add_residual(k, banks))
+            ahead = fine_product(k + 1) if k + 1 < len(pieces) else None
+            rounded_results.append(add_residual(k, banks))
             banks = ahead
+
         out_scales = keep.tile([P, S], U8, name="out_scales", tag="h2", align_bytes=64)
         result_codes = keep.tile([P, S], U32, name="result_codes", align_bytes=64)
-        for (a, b), result_rounded in zip(pieces, rounded):
+        for (a, b), result_rounded in zip(pieces, rounded_results):
             nc.vector.quantize_mx(result_codes[:, a:b].bitcast(FP8X4), out_scales[:, a:b], result_rounded[:])
             if b in word_starts:
                 nc.sync.dma_start(out_words[:, word_starts[b] : b], result_codes[:, word_starts[b] : b].bitcast(I32))
-        for q in range(4):
-            queue = nc.sync if q < 2 else nc.scalar
+        for q in range(QUADRANTS):
+            queue = nc.sync if q < QUADRANTS // 2 else nc.scalar
             queue.dma_start(out_2[0, 4 * q : 4 * q + 4, :].bitcast(I32), out_scales[32 * q : 32 * q + 4, :].bitcast(I32))

@@ -27,10 +27,8 @@ QUADRANTS = 4
 W1_LOADS = (192, 192, 128)
 PICK_PIECES = (512, 256, 256)
 FIRST_PLANE_BANKS = (256, 256, 256, 128, 128)
-LAST_PLANE_PIECES = (256, 256, 256, 256)
 POOL_PIECES = (512, 256, 256)
 FINE_PIECES = (256, 256, 256, 128, 128)
-STORED_BY_BANK = 2
 WORD_PIECES = (512, 256, 256)
 
 
@@ -126,7 +124,7 @@ def tile_picked_unet1_relu_po_kernel(
         last_pair = quantise_weight(other_rounded[:, 1:], 2 * P, "w1_last", "w1_last")
         w1_planes.extend([last_pair + (0,), last_pair + (P,)])
 
-        y = [keep.tile([P, S if t == PACK - 1 else 2 * S], F32, name="y%d" % t) for t in range(PACK)]
+        y = [keep.tile([P, S], F32, name="y%d" % t) for t in range(PACK)]
         for t, (w1_codes, w1_scales, start) in enumerate(w1_planes):
             cols = slice(start, start + P)
             for n, (a, b) in enumerate(spans(FIRST_PLANE_BANKS if t == 0 else (BANK, BANK))):
@@ -145,13 +143,19 @@ def tile_picked_unet1_relu_po_kernel(
                         )
                 relu(y[t][:, a:b], bank[:], t == 0 and n in (0, 2))
 
-        late = keep.tile([P, (PACK + 1) * S], F32, name="late", tag="late", align_bytes=64)
-        ordered = late[:, S:].rearrange("p (t c) -> p t c", t=PACK)
-        w2_rounded = late[:, :S].bitcast(BF16).rearrange("p (t m j) -> p t m j", t=PACK, j=PACK)
+        y_all = keep.tile([P, PACK, S], F32, name="y_all", align_bytes=64)
+        for t in range(PACK):
+            nc.sync.dma_start(y_all[:, t, :], y[t][:])
+
+        def gather(out, window, offsets, on_vector):
+            if on_vector:
+                nc.vector.tensor_copy(out, window.indirect(offsets))
+            else:
+                nc.scalar.activation(out, window.indirect(offsets), COPY)
+
         w2_high = load_weight_columns(w2, H // 2, (H // 2,), "w2_high", "raw_low")
-        for raw, start, a, b in ((w2_low, 0, 0, P // 4), (w2_low, 0, P // 4, P // 2), (w2_high, P // 2, 0, P // 2)):
-            nc.scalar.activation(dealt(w2_rounded[:, :, start + a : start + b, :]), by_lines(raw)[:, a:b], COPY)
-        w2_pairs = [quantise_weight(w2_rounded[:, :2], 2 * P, "w2_low", "w2_low")]
+        w2_front = keep.tile([P, 2, P, PACK], BF16, name="w2_front", align_bytes=64)
+        nc.scalar.activation(dealt(w2_front[:, :, : P // 2, :]), by_lines(w2_low)[:, :, :, :2], COPY)
 
         w3_raw = keep.tile([P, N], U32, name="w3_raw", tag="raw_high")
         nc.sync.dma_start(w3_raw[:].bitcast(I32), w3_words[0].rearrange("p n r -> p (n r)").bitcast(I32))
@@ -159,24 +163,22 @@ def tile_picked_unet1_relu_po_kernel(
         residual = keep.tile([P, PACK, S], F32, name="residual", tag="wide", align_bytes=64)
         nc.sync.dma_start(residual[:], res.rearrange("(p t) j -> p t j", t=PACK))
 
-        h = [keep.tile([P, V], F32, name="h%d" % t, align_bytes=64) for t in range(PACK)]
-        for t in range(PACK - 1):
-            nc.vector.tensor_copy(ordered[:, t, :], y[t][:].indirect(order_t[:]))
+        pools = spans(POOL_PIECES)
+        ordered = [keep.tile([P, PACK, b - a], F32, name="ordered%d" % a, align_bytes=64) for a, b in pools]
+        for t in (0, 2):
+            for piece, (a, b) in zip(ordered, pools):
+                gather(piece[:, t, :], y[t][:], entries(order_t, a, b), True)
+        for piece, (a, b) in zip(ordered, pools):
+            for t in (1, 3):
+                gather(piece[:, t, :], y[t][:], entries(order_t, a, b), False)
+        nc.vector.tensor_copy(dealt(w2_front[:, :, P // 2 :, :]), by_lines(w2_high)[:, :, :, :2])
+        w2_pairs = [quantise_weight(w2_front[:], 2 * P, "w2_low", "w2_low")]
 
-        parted = {}
-
-        def part_pairs(u, a, b):
-            start = max(begin for begin in parted if begin <= a)
-            target = parted[start][:, :, u, (a - start) // 2 : (b - start) // 2, :]
-            nc.scalar.copy(
-                target.rearrange("p e (c i) s -> p c s i e", i=LINE),
-                ordered[:, 2 * u : 2 * u + 2, a:b].rearrange("p s (c i e) -> p c s i e", i=LINE, e=2),
-            )
-
-        def largest(a, b, name):
-            z = keep.tile([P, (b - a) // 2 * PACK], BF16, name=name, align_bytes=64)
-            members = [parted[a][:, e].rearrange("p u c s -> p c u s") for e in range(2)]
-            nc.vector.tensor_tensor(z[:].rearrange("p (c u s) -> p c u s", u=2, s=2), members[0], members[1], MAX)
+        def largest(n):
+            a, b = pools[n]
+            z = keep.tile([P, (b - a) // 2 * PACK], BF16, name="z%d" % n, align_bytes=64)
+            members = ordered[n][:].rearrange("p t (c i e) -> p e c t i", i=2, e=2)
+            nc.vector.tensor_tensor(z[:].rearrange("p (c i t) -> p c t i", i=2, t=PACK), members[:, 0], members[:, 1], MAX)
             return z
 
         z_codes = keep.tile([P, V], U32, name="z_codes", align_bytes=64)
@@ -185,7 +187,9 @@ def tile_picked_unet1_relu_po_kernel(
         def quantise_z(z, a, b):
             nc.vector.quantize_mx(z_codes[:, a // 2 : b // 2].bitcast(FP8X4), z_scales[:, a // 2 : b // 2], z[:])
 
-        def coarse_product(t, a, b, on_vector=False):
+        h = [keep.tile([P, V], F32, name="h%d" % t, align_bytes=64) for t in range(PACK)]
+
+        def coarse_product(t, a, b, on_vector):
             w2_codes, w2_scales = w2_pairs[t // 2]
             cols = slice(t % 2 * P, (t % 2 + 1) * P)
             coarse = slice(a // 2, b // 2)
@@ -201,58 +205,54 @@ def tile_picked_unet1_relu_po_kernel(
             )
             relu(h[t][:, coarse], bank[:], on_vector)
 
-        first, second, last = spans(POOL_PIECES)
-        for (a, b), tag in zip((first, second, last), ("first_rounded", "picked_scales", "w1_last")):
-            parted[a] = keep.tile([P, 2, 2, (b - a) // 2, 2], BF16, name="parted%d" % a, tag=tag, align_bytes=64)
-            part_pairs(0, a, b)
-        for a, b in spans(LAST_PLANE_PIECES):
-            nc.vector.tensor_copy(ordered[:, PACK - 1, a:b], y[PACK - 1][:].indirect(entries(order_t, a, b)))
-            part_pairs(1, a, b)
-        z_first = largest(*first, "z_first")
-        z_second = largest(*second, "z_second")
+        first, second, last = pools
+        z_first = largest(0)
+        z_second = largest(1)
         quantise_z(z_first, *first)
-        z_last = largest(*last, "z_last")
         quantise_z(z_second, *second)
+        z_last = largest(2)
+        w3_codes = keep.tile([P, N], U32, name="w3_codes", tag="ordered%d" % second[0], align_bytes=64)
+        nc.vector.tensor_copy(w3_codes[:].rearrange("p (t m) -> p m t", t=PACK), w3_raw[:].rearrange("p (m t) -> p m t", t=PACK))
         quantise_z(z_last, *last)
 
-        w2_pairs.append(quantise_weight(w2_rounded[:, 2:], 2 * P, "w2_high", "z_second"))
-        w3_codes = keep.tile([P, N], U32, name="w3_codes", tag="z_last", align_bytes=64)
-        nc.vector.tensor_copy(w3_codes[:].rearrange("p (t m) -> p m t", t=PACK), w3_raw[:].rearrange("p (m t) -> p m t", t=PACK))
-        w3_planes = keep.tile([P, N], U8, name="w3_planes", tag="late", align_bytes=64)
-        nc.vector.tensor_copy(w3_planes[:].rearrange("p (t m) -> p m t", t=PACK), w3_rows[:].rearrange("p (m t) -> p m t", t=PACK))
-
-        coarse_product(0, *first)
-        coarse_product(1, *first, on_vector=True)
-        coarse_product(0, *second)
-        coarse_product(0, *last)
-        coarse_product(1, second[0], S)
+        w2_back = keep.tile([P, 2, P, PACK], BF16, name="w2_back", tag="ordered0", align_bytes=64)
+        for raw, start in ((w2_low, 0), (w2_high, P // 2)):
+            nc.scalar.activation(dealt(w2_back[:, :, start : start + P // 2, :]), by_lines(raw)[:, :, :, 2:], COPY)
+        coarse_product(0, *first, False)
+        coarse_product(1, *first, False)
+        coarse_product(0, second[0], S, True)
+        w2_pairs.append(quantise_weight(w2_back[:], 2 * P, "w2_high", "w2_high"))
+        coarse_product(1, second[0], S, True)
         for t in range(2, PACK):
-            coarse_product(t, 0, S)
+            coarse_product(t, 0, S, True)
 
         out_rows = out_0.rearrange("(p t) j -> p t j", t=PACK)
         out_words = out_1[0].rearrange("p n r -> p (n r)").bitcast(I32)
         word_starts = {b: a for a, b in spans(WORD_PIECES)}
         pieces = spans(FINE_PIECES)
-        z2_of = {}
 
-        def gather_coarse(k, t):
+        fetched = [keep.tile([P, PACK, b - a], F32, name="fetched%d" % a, align_bytes=64) for a, b in pieces]
+        for k, (a, b) in enumerate(pieces):
+            for t in range(PACK):
+                gather(fetched[k][:, t, :], h[t][:], entries(par_t, a, b), (k, t) == (0, PACK - 1))
+
+        def add_fine(k):
             a, b = pieces[k]
-            if t == 0:
-                z2_of[k] = ring.tile([P, PACK, b - a], F32, name="z2", align_bytes=64)
-            nc.vector.tensor_tensor(z2_of[k][:, t, :], h[t][:].indirect(entries(par_t, a, b)), y[t][:, a:b], ADD)
+            z2 = keep.tile([P, (b - a) * PACK], BF16, name="z2_%d" % k, align_bytes=64)
+            nc.vector.tensor_tensor(
+                z2[:].rearrange("p (c i t) -> p c t i", i=LINE, t=PACK),
+                fetched[k][:].rearrange("p t (c i) -> p c t i", i=LINE),
+                y_all[:, :, a:b].rearrange("p t (c i) -> p c t i", i=LINE),
+                ADD,
+            )
+            return z2
 
-        def fine_product(k):
+        def fine_product(k, z2):
             a, b = pieces[k]
             width = b - a
-            for t in range(PACK):
-                if (k, t) != (1, 0):
-                    gather_coarse(k, t)
-                if (k, t) == (0, 0):
-                    gather_coarse(1, 0)
-            z2_rounded = round_interleaved(z2_of[k], width, "z2_rounded", 2, False)
-            z2_codes = ring.tile([P, width], U32, name="z2_codes", align_bytes=64)
-            z2_scales = ring.tile([P, width], U8, name="z2_scales", align_bytes=64)
-            nc.vector.quantize_mx(z2_codes[:].bitcast(FP8X4), z2_scales[:], z2_rounded[:])
+            z2_codes = keep.tile([P, width], U32, name="z2_codes%d" % k, align_bytes=64)
+            z2_scales = keep.tile([P, width], U8, name="z2_scales%d" % k, align_bytes=64)
+            nc.vector.quantize_mx(z2_codes[:].bitcast(FP8X4), z2_scales[:], z2[:])
             per_bank = 2 if b == S else BANK // width
             banks = []
             for t0 in range(0, PACK, per_bank):
@@ -273,25 +273,26 @@ def tile_picked_unet1_relu_po_kernel(
 
         def add_residual(k, banks):
             a, b = pieces[k]
-            result = ring.tile([P, PACK, b - a], F32, name="result", bufs=len(pieces))
+            result = keep.tile([P, PACK, b - a], F32, name="result%d" % k, align_bytes=64)
             for planes, bank in banks:
                 nc.vector.tensor_tensor(result[:, planes, :], bank[:], residual[:, planes, a:b], ADD)
-                if k == STORED_BY_BANK:
-                    nc.sync.dma_start(out_rows[:, planes, a:b], result[:, planes, :])
-            if k != STORED_BY_BANK:
-                nc.sync.dma_start(out_rows[:, :, a:b], result[:])
-            return round_interleaved(result, b - a, "result_rounded", len(pieces), b == S)
+            nc.sync.dma_start(out_rows[:, :, a:b], result[:])
+            return result
 
-        banks = fine_product(0)
-        rounded_results = []
+        z2 = add_fine(0)
+        w3_planes = keep.tile([P, N], U8, name="w3_planes", tag="z2", align_bytes=64)
+        nc.vector.tensor_copy(w3_planes[:].rearrange("p (t m) -> p m t", t=PACK), w3_rows[:].rearrange("p (m t) -> p m t", t=PACK))
+        results = []
         for k in range(len(pieces)):
-            ahead = fine_product(k + 1) if k + 1 < len(pieces) else None
-            rounded_results.append(add_residual(k, banks))
-            banks = ahead
+            banks = fine_product(k, z2)
+            if k + 1 < len(pieces):
+                z2 = add_fine(k + 1)
+            results.append(add_residual(k, banks))
 
-        out_scales = keep.tile([P, S], U8, name="out_scales", tag="h2", align_bytes=64)
+        out_scales = keep.tile([P, S], U8, name="out_scales", tag="fetched%d" % pieces[-1][0], align_bytes=64)
         result_codes = keep.tile([P, S], U32, name="result_codes", align_bytes=64)
-        for (a, b), result_rounded in zip(pieces, rounded_results):
+        for (a, b), result in zip(pieces, results):
+            result_rounded = round_interleaved(result, b - a, "result_rounded", len(pieces), b == S)
             nc.vector.quantize_mx(result_codes[:, a:b].bitcast(FP8X4), out_scales[:, a:b], result_rounded[:])
             if b in word_starts:
                 nc.sync.dma_start(out_words[:, word_starts[b] : b], result_codes[:, word_starts[b] : b].bitcast(I32))

@@ -153,25 +153,29 @@ def tile_picked_unet1_relu_po_kernel(
             else:
                 nc.scalar.activation(out, window.indirect(offsets), COPY)
 
-        w2_high = load_weight_columns(w2, H // 2, (H // 2,), "w2_high", "raw_low")
+        w2_high = load_weight_columns(w2, H // 2, (H // 2,), "w2_high", "w2_raw_high")
         w2_front = keep.tile([P, 2, P, PACK], BF16, name="w2_front", align_bytes=64)
-        nc.scalar.activation(dealt(w2_front[:, :, : P // 2, :]), by_lines(w2_low)[:, :, :, :2], COPY)
+        for raw, start in ((w2_low, 0), (w2_high, P // 2)):
+            nc.scalar.activation(dealt(w2_front[:, :, start : start + P // 2, :]), by_lines(raw)[:, :, :, :2], COPY)
 
-        w3_raw = keep.tile([P, N], U32, name="w3_raw", tag="raw_high")
+        w3_raw = keep.tile([P, N], U32, name="w3_raw")
         nc.sync.dma_start(w3_raw[:].bitcast(I32), w3_words[0].rearrange("p n r -> p (n r)").bitcast(I32))
         w3_rows = load_scale_rows(w3_scales, N, "w3_rows")
-        residual = keep.tile([P, PACK, S], F32, name="residual", tag="wide", align_bytes=64)
-        nc.sync.dma_start(residual[:], res.rearrange("(p t) j -> p t j", t=PACK))
+        pieces = spans(FINE_PIECES)
+        residual = {}
+        for k, (a, b) in enumerate(pieces):
+            for u in range(2):
+                residual[k, u] = keep.tile([P, 2, b - a], F32, name="residual%d_%d" % (k, u), align_bytes=64)
+                nc.sync.dma_start(residual[k, u][:], res.rearrange("(p t) j -> p t j", t=PACK)[:, 2 * u : 2 * u + 2, a:b])
 
         pools = spans(POOL_PIECES)
         ordered = [keep.tile([P, PACK, b - a], F32, name="ordered%d" % a, align_bytes=64) for a, b in pools]
-        for t in (0, 2):
+        for t in (0, 1):
             for piece, (a, b) in zip(ordered, pools):
                 gather(piece[:, t, :], y[t][:], entries(order_t, a, b), True)
         for piece, (a, b) in zip(ordered, pools):
-            for t in (1, 3):
-                gather(piece[:, t, :], y[t][:], entries(order_t, a, b), False)
-        nc.vector.tensor_copy(dealt(w2_front[:, :, P // 2 :, :]), by_lines(w2_high)[:, :, :, :2])
+            for t in (2, 3):
+                gather(piece[:, t, :], y[t][:], entries(order_t, a, b), (a, t) == (0, 2))
         w2_pairs = [quantise_weight(w2_front[:], 2 * P, "w2_low", "w2_low")]
 
         def largest(n):
@@ -229,16 +233,17 @@ def tile_picked_unet1_relu_po_kernel(
         out_rows = out_0.rearrange("(p t) j -> p t j", t=PACK)
         out_words = out_1[0].rearrange("p n r -> p (n r)").bitcast(I32)
         word_starts = {b: a for a, b in spans(WORD_PIECES)}
-        pieces = spans(FINE_PIECES)
 
         fetched = [keep.tile([P, PACK, b - a], F32, name="fetched%d" % a, align_bytes=64) for a, b in pieces]
         for k, (a, b) in enumerate(pieces):
             for t in range(PACK):
-                gather(fetched[k][:, t, :], h[t][:], entries(par_t, a, b), (k, t) == (0, PACK - 1))
+                if (k, t) != (1, PACK - 1):
+                    gather(fetched[k][:, t, :], h[t][:], entries(par_t, a, b), (k, t) == (0, PACK - 1))
+
 
         def add_fine(k):
             a, b = pieces[k]
-            z2 = keep.tile([P, (b - a) * PACK], BF16, name="z2_%d" % k, align_bytes=64)
+            z2 = keep.tile([P, (b - a) * PACK], BF16, name="z2_%d" % k, tag="residual%d_1" % (k - 2) if k >= 2 else "z2_%d" % k, align_bytes=64)
             nc.vector.tensor_tensor(
                 z2[:].rearrange("p (c i t) -> p c t i", i=LINE, t=PACK),
                 fetched[k][:].rearrange("p t (c i) -> p c t i", i=LINE),
@@ -250,10 +255,10 @@ def tile_picked_unet1_relu_po_kernel(
         def fine_product(k, z2):
             a, b = pieces[k]
             width = b - a
-            z2_codes = keep.tile([P, width], U32, name="z2_codes%d" % k, align_bytes=64)
+            z2_codes = keep.tile([P, width], U32, name="z2_codes%d" % k, tag="residual%d_0" % (k - 1) if k >= 1 else "z2_codes0", align_bytes=64)
             z2_scales = keep.tile([P, width], U8, name="z2_scales%d" % k, align_bytes=64)
             nc.vector.quantize_mx(z2_codes[:].bitcast(FP8X4), z2_scales[:], z2[:])
-            per_bank = 2 if b == S else BANK // width
+            per_bank = 2
             banks = []
             for t0 in range(0, PACK, per_bank):
                 bank = psum.tile([P, per_bank, width], F32, name="bank")
@@ -274,8 +279,8 @@ def tile_picked_unet1_relu_po_kernel(
         def add_residual(k, banks):
             a, b = pieces[k]
             result = keep.tile([P, PACK, b - a], F32, name="result%d" % k, align_bytes=64)
-            for planes, bank in banks:
-                nc.vector.tensor_tensor(result[:, planes, :], bank[:], residual[:, planes, a:b], ADD)
+            for u, (planes, bank) in enumerate(banks):
+                nc.vector.tensor_tensor(result[:, planes, :], bank[:], residual[k, u][:], ADD)
             nc.sync.dma_start(out_rows[:, :, a:b], result[:])
             return result
 
@@ -285,11 +290,13 @@ def tile_picked_unet1_relu_po_kernel(
         results = []
         for k in range(len(pieces)):
             banks = fine_product(k, z2)
+            if k == 0:
+                gather(fetched[1][:, PACK - 1, :], h[PACK - 1][:], entries(par_t, *pieces[1]), True)
             if k + 1 < len(pieces):
                 z2 = add_fine(k + 1)
             results.append(add_residual(k, banks))
 
-        out_scales = keep.tile([P, S], U8, name="out_scales", tag="fetched%d" % pieces[-1][0], align_bytes=64)
+        out_scales = keep.tile([P, S], U8, name="out_scales", tag="residual3_1", align_bytes=64)
         result_codes = keep.tile([P, S], U32, name="result_codes", align_bytes=64)
         for (a, b), result in zip(pieces, results):
             result_rounded = round_interleaved(result, b - a, "result_rounded", len(pieces), b == S)

@@ -88,7 +88,7 @@ def tile_picked_unet1_relu_po_kernel(
         def round_interleaved(values, width, name, bufs, on_vector):
             rounded = ring.tile([P, width * PACK], BF16, name=name, align_bytes=64, bufs=bufs)
             target = rounded[:].rearrange("p (c i t) -> p c t i", i=LINE, t=PACK)
-            source = values[:].rearrange("p t (c i) -> p c t i", i=LINE)
+            source = values.rearrange("p t (c i) -> p c t i", i=LINE)
             if on_vector:
                 nc.vector.tensor_copy(target, source)
             else:
@@ -143,9 +143,13 @@ def tile_picked_unet1_relu_po_kernel(
                         )
                 relu(y[t][:, a:b], bank[:], t == 0 and n in (0, 2))
 
-        y_all = keep.tile([P, PACK, S], F32, name="y_all", align_bytes=64)
-        for t in range(PACK):
-            nc.sync.dma_start(y_all[:, t, :], y[t][:])
+        pieces = spans(FINE_PIECES)
+        fused = (pieces[1][0], pieces[2][1])
+        y_all = {}
+        for name, (a, b) in (("y_head", (0, fused[0])), ("y_tail", (fused[1], S))):
+            y_all[a] = keep.tile([P, PACK, b - a], F32, name=name, align_bytes=64)
+            for t in range(PACK):
+                nc.sync.dma_start(y_all[a][:, t, :], y[t][:, a:b])
 
         def gather(out, window, offsets, on_vector):
             if on_vector:
@@ -161,7 +165,6 @@ def tile_picked_unet1_relu_po_kernel(
         w3_raw = keep.tile([P, N], U32, name="w3_raw")
         nc.sync.dma_start(w3_raw[:].bitcast(I32), w3_words[0].rearrange("p n r -> p (n r)").bitcast(I32))
         w3_rows = load_scale_rows(w3_scales, N, "w3_rows")
-        pieces = spans(FINE_PIECES)
         residual = {}
         for k, (a, b) in enumerate(pieces):
             for u in range(2):
@@ -191,7 +194,7 @@ def tile_picked_unet1_relu_po_kernel(
         def quantise_z(z, a, b):
             nc.vector.quantize_mx(z_codes[:, a // 2 : b // 2].bitcast(FP8X4), z_scales[:, a // 2 : b // 2], z[:])
 
-        h = [keep.tile([P, V], F32, name="h%d" % t, align_bytes=64) for t in range(PACK)]
+        h = [keep.tile([P, 2 * V], F32, name="h%d" % t, align_bytes=64) for t in range(PACK)]
 
         def coarse_product(t, a, b, on_vector):
             w2_codes, w2_scales = w2_pairs[t // 2]
@@ -224,38 +227,38 @@ def tile_picked_unet1_relu_po_kernel(
             nc.scalar.activation(dealt(w2_back[:, :, start : start + P // 2, :]), by_lines(raw)[:, :, :, 2:], COPY)
         coarse_product(0, *first, False)
         coarse_product(1, *first, False)
-        coarse_product(0, second[0], S, True)
         w2_pairs.append(quantise_weight(w2_back[:], 2 * P, "w2_high", "w2_high"))
-        coarse_product(1, second[0], S, True)
+        coarse_product(0, second[0], S, True)
+        coarse_product(1, second[0], S, False)
         for t in range(2, PACK):
-            coarse_product(t, 0, S, True)
+            coarse_product(t, 0, S, False)
 
         out_rows = out_0.rearrange("(p t) j -> p t j", t=PACK)
         out_words = out_1[0].rearrange("p n r -> p (n r)").bitcast(I32)
         word_starts = {b: a for a, b in spans(WORD_PIECES)}
 
-        fetched = [keep.tile([P, PACK, b - a], F32, name="fetched%d" % a, align_bytes=64) for a, b in pieces]
-        for k, (a, b) in enumerate(pieces):
+        def fetch(a, b, tag):
+            fetched = keep.tile([P, PACK, b - a], F32, name="fetched%d" % a, tag=tag, align_bytes=64)
             for t in range(PACK):
-                if (k, t) != (1, PACK - 1):
-                    gather(fetched[k][:, t, :], h[t][:], entries(par_t, a, b), (k, t) == (0, PACK - 1))
+                gather(fetched[:, t, :], h[t][:], entries(par_t, a, b), False)
+            return fetched
 
-
-        def add_fine(k):
+        def add_fine(k, fetched, tag):
             a, b = pieces[k]
-            z2 = keep.tile([P, (b - a) * PACK], BF16, name="z2_%d" % k, tag="residual%d_1" % (k - 2) if k >= 2 else "z2_%d" % k, align_bytes=64)
+            start = max(begin for begin in y_all if begin <= a)
+            z2 = keep.tile([P, (b - a) * PACK], BF16, name="z2_%d" % k, tag=tag, align_bytes=64)
             nc.vector.tensor_tensor(
                 z2[:].rearrange("p (c i t) -> p c t i", i=LINE, t=PACK),
-                fetched[k][:].rearrange("p t (c i) -> p c t i", i=LINE),
-                y_all[:, :, a:b].rearrange("p t (c i) -> p c t i", i=LINE),
+                fetched[:, :, a - start : b - start].rearrange("p t (c i) -> p c t i", i=LINE),
+                y_all[start][:, :, a - start : b - start].rearrange("p t (c i) -> p c t i", i=LINE),
                 ADD,
             )
             return z2
 
-        def fine_product(k, z2):
+        def fine_product(k, z2, tag):
             a, b = pieces[k]
             width = b - a
-            z2_codes = keep.tile([P, width], U32, name="z2_codes%d" % k, tag="residual%d_0" % (k - 1) if k >= 1 else "z2_codes0", align_bytes=64)
+            z2_codes = keep.tile([P, width], U32, name="z2_codes%d" % k, tag=tag, align_bytes=64)
             z2_scales = keep.tile([P, width], U8, name="z2_scales%d" % k, align_bytes=64)
             nc.vector.quantize_mx(z2_codes[:].bitcast(FP8X4), z2_scales[:], z2[:])
             per_bank = 2
@@ -284,22 +287,26 @@ def tile_picked_unet1_relu_po_kernel(
             nc.sync.dma_start(out_rows[:, :, a:b], result[:])
             return result
 
-        z2 = add_fine(0)
-        w3_planes = keep.tile([P, N], U8, name="w3_planes", tag="z2", align_bytes=64)
+        sums = keep.tile([P, PACK, fused[1] - fused[0]], F32, name="sums", align_bytes=64)
+        for t in range(PACK):
+            nc.vector.tensor_tensor(sums[:, t, :], h[t][:].indirect(entries(par_t, *fused)), y[t][:, fused[0] : fused[1]], ADD)
+        fetched = fetch(0, fused[0], "fetched0")
+        z2 = {k: round_interleaved(sums[:, :, pieces[k][0] - fused[0] : pieces[k][1] - fused[0]], FINE_PIECES[k], "z2_rounded", 2, False) for k in (1, 2)}
+        z2[0] = add_fine(0, fetched, "z2_0")
+        w3_planes = keep.tile([P, N], U8, name="w3_planes", tag="z_codes", align_bytes=64)
         nc.vector.tensor_copy(w3_planes[:].rearrange("p (t m) -> p m t", t=PACK), w3_rows[:].rearrange("p (m t) -> p m t", t=PACK))
-        results = []
-        for k in range(len(pieces)):
-            banks = fine_product(k, z2)
-            if k == 0:
-                gather(fetched[1][:, PACK - 1, :], h[PACK - 1][:], entries(par_t, *pieces[1]), True)
-            if k + 1 < len(pieces):
-                z2 = add_fine(k + 1)
-            results.append(add_residual(k, banks))
+        banks = {k: fine_product(k, z2[k], "z2_codes%d" % k) for k in range(3)}
+        fetched = fetch(fused[1], S, "sums")
+        results = [add_residual(k, banks[k]) for k in range(3)]
+        z2[3] = add_fine(3, fetched, "residual2_0")
+        z2[4] = add_fine(4, fetched, "residual1_1")
+        banks = {k: fine_product(k, z2[k], "z2_codes%d" % k) for k in (3, 4)}
+        results.extend(add_residual(k, banks[k]) for k in (3, 4))
 
-        out_scales = keep.tile([P, S], U8, name="out_scales", tag="residual3_1", align_bytes=64)
+        out_scales = keep.tile([P, S], U8, name="out_scales", tag="sums", align_bytes=64)
         result_codes = keep.tile([P, S], U32, name="result_codes", align_bytes=64)
         for (a, b), result in zip(pieces, results):
-            result_rounded = round_interleaved(result, b - a, "result_rounded", len(pieces), b == S)
+            result_rounded = round_interleaved(result[:], b - a, "result_rounded", len(pieces), b == S)
             nc.vector.quantize_mx(result_codes[:, a:b].bitcast(FP8X4), out_scales[:, a:b], result_rounded[:])
             if b in word_starts:
                 nc.sync.dma_start(out_words[:, word_starts[b] : b], result_codes[:, word_starts[b] : b].bitcast(I32))

@@ -144,9 +144,9 @@ def tile_picked_unet1_relu_po_kernel(
                 relu(y[t][:, a:b], bank[:], t == 0 and n in (0, 2))
 
         pieces = spans(FINE_PIECES)
-        fused = (pieces[1][0], pieces[2][1])
+        fused = (pieces[0][0], pieces[1][1])
         y_all = {}
-        for name, (a, b) in (("y_head", (0, fused[0])), ("y_tail", (fused[1], S))):
+        for name, (a, b) in (("y_head", pieces[2]), ("y_tail", (pieces[3][0], S))):
             y_all[a] = keep.tile([P, PACK, b - a], F32, name=name, align_bytes=64)
             for t in range(PACK):
                 nc.sync.dma_start(y_all[a][:, t, :], y[t][:, a:b])
@@ -172,7 +172,7 @@ def tile_picked_unet1_relu_po_kernel(
                 nc.sync.dma_start(residual[k, u][:], res.rearrange("(p t) j -> p t j", t=PACK)[:, 2 * u : 2 * u + 2, a:b])
 
         pools = spans(POOL_PIECES)
-        ordered = [keep.tile([P, PACK, b - a], F32, name="ordered%d" % a, align_bytes=64) for a, b in pools]
+        ordered = [keep.tile([P, PACK, b - a], BF16, name="ordered%d" % a, align_bytes=64) for a, b in pools]
         for t in (0, 1):
             for piece, (a, b) in zip(ordered, pools):
                 gather(piece[:, t, :], y[t][:], entries(order_t, a, b), True)
@@ -184,8 +184,8 @@ def tile_picked_unet1_relu_po_kernel(
         def largest(n):
             a, b = pools[n]
             z = keep.tile([P, (b - a) // 2 * PACK], BF16, name="z%d" % n, align_bytes=64)
-            members = ordered[n][:].rearrange("p t (c i e) -> p e c t i", i=2, e=2)
-            nc.vector.tensor_tensor(z[:].rearrange("p (c i t) -> p c t i", i=2, t=PACK), members[:, 0], members[:, 1], MAX)
+            members = ordered[n][:].rearrange("p t (c i e) -> p e c t i", i=LINE, e=2)
+            nc.vector.tensor_tensor(z[:].rearrange("p (c i t) -> p c t i", i=LINE, t=PACK), members[:, 0], members[:, 1], MAX)
             return z
 
         z_codes = keep.tile([P, V], U32, name="z_codes", align_bytes=64)
@@ -243,17 +243,14 @@ def tile_picked_unet1_relu_po_kernel(
                 gather(fetched[:, t, :], h[t][:], entries(par_t, a, b), False)
             return fetched
 
-        def add_fine(k, fetched, tag):
-            a, b = pieces[k]
+        def add_fine(z2, fetched, a, b):
             start = max(begin for begin in y_all if begin <= a)
-            z2 = keep.tile([P, (b - a) * PACK], BF16, name="z2_%d" % k, tag=tag, align_bytes=64)
             nc.vector.tensor_tensor(
-                z2[:].rearrange("p (c i t) -> p c t i", i=LINE, t=PACK),
+                z2.rearrange("p (c i t) -> p c t i", i=LINE, t=PACK),
                 fetched[:, :, a - start : b - start].rearrange("p t (c i) -> p c t i", i=LINE),
                 y_all[start][:, :, a - start : b - start].rearrange("p t (c i) -> p c t i", i=LINE),
                 ADD,
             )
-            return z2
 
         def fine_product(k, z2, tag):
             a, b = pieces[k]
@@ -290,16 +287,21 @@ def tile_picked_unet1_relu_po_kernel(
         sums = keep.tile([P, PACK, fused[1] - fused[0]], F32, name="sums", align_bytes=64)
         for t in range(PACK):
             nc.vector.tensor_tensor(sums[:, t, :], h[t][:].indirect(entries(par_t, *fused)), y[t][:, fused[0] : fused[1]], ADD)
-        fetched = fetch(0, fused[0], "fetched0")
-        z2 = {k: round_interleaved(sums[:, :, pieces[k][0] - fused[0] : pieces[k][1] - fused[0]], FINE_PIECES[k], "z2_rounded", 2, False) for k in (1, 2)}
-        z2[0] = add_fine(0, fetched, "z2_0")
+        fetched = fetch(*pieces[2], "w2_high")
         w3_planes = keep.tile([P, N], U8, name="w3_planes", tag="z_codes", align_bytes=64)
         nc.vector.tensor_copy(w3_planes[:].rearrange("p (t m) -> p m t", t=PACK), w3_rows[:].rearrange("p (m t) -> p m t", t=PACK))
-        banks = {k: fine_product(k, z2[k], "z2_codes%d" % k) for k in range(3)}
-        fetched = fetch(fused[1], S, "sums")
+        z2 = {k: round_interleaved(sums[:, :, pieces[k][0] - fused[0] : pieces[k][1] - fused[0]], FINE_PIECES[k], "z2_rounded", 2, k == 0) for k in (0, 1)}
+        a, b = pieces[2]
+        z2[2] = keep.tile([P, (b - a) * PACK], BF16, name="z2_2", align_bytes=64)
+        add_fine(z2[2][:, : (b - a) * 2], fetched, a, (a + b) // 2)
+        banks = {0: fine_product(0, z2[0], "z2_codes0")}
+        add_fine(z2[2][:, (b - a) * 2 :], fetched, (a + b) // 2, b)
+        banks.update({k: fine_product(k, z2[k], "z2_codes%d" % k) for k in (1, 2)})
+        fetched = fetch(pieces[3][0], S, "sums")
         results = [add_residual(k, banks[k]) for k in range(3)]
-        z2[3] = add_fine(3, fetched, "residual2_0")
-        z2[4] = add_fine(4, fetched, "residual1_1")
+        for k, tag in ((3, "residual2_0"), (4, "residual1_1")):
+            z2[k] = keep.tile([P, FINE_PIECES[k] * PACK], BF16, name="z2_%d" % k, tag=tag, align_bytes=64)
+            add_fine(z2[k][:], fetched, *pieces[k])
         banks = {k: fine_product(k, z2[k], "z2_codes%d" % k) for k in (3, 4)}
         results.extend(add_residual(k, banks[k]) for k in (3, 4))
 

@@ -29,7 +29,7 @@ PICK_PIECES = (512, 256, 256)
 FIRST_PLANE_BANKS = (256, 256, 256, 128, 128)
 POOL_PIECES = (512, 256, 256)
 FINE_PIECES = (256, 256, 256, 128, 128)
-WORD_PIECES = (512, 256, 256)
+WORD_PIECES = (768, 256)
 
 
 def spans(widths):
@@ -228,6 +228,8 @@ def tile_picked_unet1_relu_po_kernel(
         coarse_product(0, *first, False)
         coarse_product(1, *first, False)
         w2_pairs.append(quantise_weight(w2_back[:], 2 * P, "w2_high", "w2_high"))
+        w3_planes = keep.tile([P, N], U8, name="w3_planes", tag="z1", align_bytes=64)
+        nc.vector.tensor_copy(w3_planes[:].rearrange("p (t m) -> p m t", t=PACK), w3_rows[:].rearrange("p (m t) -> p m t", t=PACK))
         coarse_product(0, second[0], S, True)
         coarse_product(1, second[0], S, False)
         for t in range(2, PACK):
@@ -281,15 +283,17 @@ def tile_picked_unet1_relu_po_kernel(
             result = keep.tile([P, PACK, b - a], F32, name="result%d" % k, align_bytes=64)
             for u, (planes, bank) in enumerate(banks):
                 nc.vector.tensor_tensor(result[:, planes, :], bank[:], residual[k, u][:], ADD)
-            nc.sync.dma_start(out_rows[:, :, a:b], result[:])
+                if k == 0:
+                    nc.sync.dma_start(out_rows[:, planes, a:b], result[:, planes, :])
+            if k != 0:
+                nc.sync.dma_start(out_rows[:, :, a:b], result[:])
             return result
 
         sums = keep.tile([P, PACK, fused[1] - fused[0]], F32, name="sums", align_bytes=64)
         for t in range(PACK):
-            nc.vector.tensor_tensor(sums[:, t, :], h[t][:].indirect(entries(par_t, *fused)), y[t][:, fused[0] : fused[1]], ADD)
-        fetched = fetch(*pieces[2], "w2_high")
-        w3_planes = keep.tile([P, N], U8, name="w3_planes", tag="z_codes", align_bytes=64)
-        nc.vector.tensor_copy(w3_planes[:].rearrange("p (t m) -> p m t", t=PACK), w3_rows[:].rearrange("p (m t) -> p m t", t=PACK))
+            for a, b in pieces[:2] if t == PACK - 1 else (fused,):
+                nc.vector.tensor_tensor(sums[:, t, a:b], h[t][:].indirect(entries(par_t, a, b)), y[t][:, a:b], ADD)
+        fetched = fetch(*pieces[2], "w2_low")
         z2 = {k: round_interleaved(sums[:, :, pieces[k][0] - fused[0] : pieces[k][1] - fused[0]], FINE_PIECES[k], "z2_rounded", 2, k == 0) for k in (0, 1)}
         a, b = pieces[2]
         z2[2] = keep.tile([P, (b - a) * PACK], BF16, name="z2_2", align_bytes=64)

@@ -157,18 +157,19 @@ def tile_picked_unet1_relu_po_kernel(
             else:
                 nc.scalar.activation(out, window.indirect(offsets), COPY)
 
-        w2_high = load_weight_columns(w2, H // 2, (H // 2,), "w2_high", "w2_raw_high")
+        w2_high = load_weight_columns(w2, H // 2, (H // 2,), "w2_high", "raw_low")
         w2_front = keep.tile([P, 2, P, PACK], BF16, name="w2_front", align_bytes=64)
         for raw, start in ((w2_low, 0), (w2_high, P // 2)):
             nc.scalar.activation(dealt(w2_front[:, :, start : start + P // 2, :]), by_lines(raw)[:, :, :, :2], COPY)
 
-        w3_raw = keep.tile([P, N], U32, name="w3_raw")
+        w3_raw = keep.tile([P, N], U32, name="w3_raw", tag="raw_high")
         nc.sync.dma_start(w3_raw[:].bitcast(I32), w3_words[0].rearrange("p n r -> p (n r)").bitcast(I32))
         w3_rows = load_scale_rows(w3_scales, N, "w3_rows")
         residual = {}
+        freed = ("wide", "rounded", "w1_first", "w1_first_scales", "w1_second", "w1_second_scales", "picked0", "picked512", "w1_last", "picked_scales")
         for k, (a, b) in enumerate(pieces):
             for u in range(2):
-                residual[k, u] = keep.tile([P, 2, b - a], F32, name="residual%d_%d" % (k, u), align_bytes=64)
+                residual[k, u] = keep.tile([P, 2, b - a], F32, name="residual%d_%d" % (k, u), tag=freed[2 * k + u], align_bytes=64)
                 nc.sync.dma_start(residual[k, u][:], res.rearrange("(p t) j -> p t j", t=PACK)[:, 2 * u : 2 * u + 2, a:b])
 
         pools = spans(POOL_PIECES)
@@ -303,7 +304,7 @@ def tile_picked_unet1_relu_po_kernel(
         banks.update({k: fine_product(k, z2[k], "z2_codes%d" % k) for k in (1, 2)})
         fetched = fetch(pieces[3][0], S, "sums")
         results = [add_residual(k, banks[k]) for k in range(3)]
-        for k, tag in ((3, "residual2_0"), (4, "residual1_1")):
+        for k, tag in ((3, freed[4]), (4, freed[3])):
             z2[k] = keep.tile([P, FINE_PIECES[k] * PACK], BF16, name="z2_%d" % k, tag=tag, align_bytes=64)
             add_fine(z2[k][:], fetched, *pieces[k])
         banks = {k: fine_product(k, z2[k], "z2_codes%d" % k) for k in (3, 4)}

@@ -227,13 +227,12 @@ def tile_picked_unet1_relu_po_kernel(
         for raw, start in ((w2_low, 0), (w2_high, P // 2)):
             nc.scalar.activation(dealt(w2_back[:, :, start : start + P // 2, :]), by_lines(raw)[:, :, :, 2:], COPY)
         coarse_product(0, *first, False)
-        coarse_product(1, *first, False)
         w2_pairs.append(quantise_weight(w2_back[:], 2 * P, "w2_high", "w2_high"))
         w3_planes = keep.tile([P, N], U8, name="w3_planes", tag="z1", align_bytes=64)
         nc.vector.tensor_copy(w3_planes[:].rearrange("p (t m) -> p m t", t=PACK), w3_rows[:].rearrange("p (m t) -> p m t", t=PACK))
-        coarse_product(0, second[0], S, True)
-        coarse_product(1, second[0], S, False)
-        for t in range(2, PACK):
+        coarse_product(0, *second, False)
+        coarse_product(0, *last, False)
+        for t in range(1, PACK):
             coarse_product(t, 0, S, False)
 
         out_rows = out_0.rearrange("(p t) j -> p t j", t=PACK)

from contextlib import ExitStack

import concourse.mybir as mybir

K, T, S, V, N, H = 512, 2048, 1024, 512, 512, 512
FLOPS = 2 * K * H * S + 2 * H * H * V + 2 * H * N * S

F32 = mybir.dt.float32
BF16 = mybir.dt.bfloat16
I32 = mybir.dt.int32
U32 = mybir.dt.uint32
U16 = mybir.dt.uint16
U8 = mybir.dt.uint8
FP8X4 = mybir.dt.float8_e4m3fn_x4
RELU = mybir.ActivationFunctionType.Relu
COPY = mybir.ActivationFunctionType.Copy
ADD = mybir.AluOpType.add
MAX = mybir.AluOpType.max

P = 128
PACK = 4
LANES = 16
BANK = 512
LINE = 4
QUADRANTS = 4

W1_LOADS = (192, 192, 128)
PICK_PIECES = (512, 256, 256)
FIRST_PLANE_BANKS = (256, 256, 256, 128, 128)
POOL_PIECES = (512, 256, 256)
FINE_PIECES = (256, 256, 256, 128, 128)
WORD_PIECES = (768, 256)


def spans(widths):
    return [(sum(widths[:i]), sum(widths[: i + 1])) for i in range(len(widths))]


def tile_picked_unet1_relu_po_kernel(
    tc, x_words, x_scales, w1, w2, res, w3_words, w3_scales, offs, order, par, out_0, out_1, out_2
):
    nc = tc.nc
    with ExitStack() as ctx:
        lists = ctx.enter_context(tc.tile_pool(name="lists", bufs=1))
        keep = ctx.enter_context(tc.tile_pool(name="keep", bufs=1))
        ring = ctx.enter_context(tc.tile_pool(name="ring", bufs=2))
        psum = ctx.enter_context(tc.psum_pool(name="psum", bufs=8))

        def load_list(source, name):
            held = lists.tile([P, S // LANES], U16, name=name)
            nc.sync.dma_start(held[:], source)
            return held

        def entries(held, a, b):
            return held[:, a // LANES : b // LANES]

        def load_scale_rows(source, width, name):
            rows = keep.tile([P, width], U8, name=name, align_bytes=64)
            nc.vector.memset(rows[:].bitcast(I32), 0)
            for q in range(QUADRANTS):
                nc.sync.dma_start(rows[32 * q : 32 * q + 4, :].bitcast(I32), source[0, 4 * q : 4 * q + 4, :].bitcast(I32))
            return rows

        def load_weight_columns(w, start, parts, name, tag):
            raw = keep.tile([P, PACK, sum(parts)], F32, name=name, tag=tag)
            for a, b in spans(parts):
                nc.sync.dma_start(raw[:, :, a:b], w.rearrange("(p j) c -> p j c", j=PACK)[:, :, start + a : start + b])
            return raw

        def dealt(rounded):
            return rounded.rearrange("p t m j -> p m j t")

        def by_lines(raw):
            return raw[:].rearrange("p j (m t) -> p m j t", t=PACK)

        def quantise_weight(rounded, width, name, tag):
            codes = keep.tile([P, width], U32, name=name + "_codes", tag=tag, align_bytes=64)
            scales = keep.tile([P, width], U8, name=name + "_scales", align_bytes=64)
            nc.vector.quantize_mx(codes[:].bitcast(FP8X4), scales[:], rounded.rearrange("p t m j -> p (t m j)"))
            return codes, scales

        def relu(out, bank, on_vector):
            if on_vector:
                nc.vector.tensor_scalar_max(out, bank, 0.0)
            else:
                nc.scalar.activation(out, bank, RELU)

        def round_interleaved(values, width, name, bufs, on_vector):
            rounded = ring.tile([P, width * PACK], BF16, name=name, align_bytes=64, bufs=bufs)
            target = rounded[:].rearrange("p (c i t) -> p c t i", i=LINE, t=PACK)
            source = values.rearrange("p t (c i) -> p c t i", i=LINE)
            if on_vector:
                nc.vector.tensor_copy(target, source)
            else:
                nc.scalar.activation(target, source, COPY)
            return rounded

        w1_low = load_weight_columns(w1, 0, W1_LOADS[:1], "w1_low", "raw_low")
        offs_t = load_list(offs, "offs_t")
        x_rows = load_scale_rows(x_scales, T, "x_rows")
        x_table = keep.tile([P, T], U32, name="x_table", tag="wide", align_bytes=64)
        nc.sync.dma_start(x_table[:].bitcast(I32), x_words[0].rearrange("p n r -> p (n r)").bitcast(I32))
        w1_high = load_weight_columns(w1, W1_LOADS[0], W1_LOADS[1:], "w1_high", "raw_high")
        w2_low = load_weight_columns(w2, 0, (H // 2,), "w2_low", "w2_raw_low")
        order_t = load_list(order, "order_t")
        par_t = load_list(par, "par_t")

        picked_scales = keep.tile([P, S], U8, name="picked_scales", align_bytes=64)
        nc.vector.tensor_copy(picked_scales[:], x_rows[:].indirect(offs_t[:]))
        first_rounded = keep.tile([P, 1, P, PACK], BF16, name="first_rounded", align_bytes=64)
        other_rounded = keep.tile([P, PACK - 1, P, PACK], BF16, name="other_rounded", tag="rounded", align_bytes=64)
        for raw, start, parts in ((w1_low, 0, W1_LOADS[:1]), (w1_high, W1_LOADS[0] // PACK, W1_LOADS[1:])):
            for a, b in spans([part // PACK for part in parts]):
                nc.scalar.activation(dealt(first_rounded[:, :, start + a : start + b, :]), by_lines(raw)[:, a:b, :, :1], COPY)
            nc.scalar.activation(dealt(other_rounded[:, :, start : start + sum(parts) // PACK, :]), by_lines(raw)[:, :, :, 1:], COPY)
        w1_planes = [quantise_weight(first_rounded[:], P, "w1_first", "w1_first") + (0,)]
        picked = []
        for a, b in spans(PICK_PIECES):
            tag = "first_rounded" if b == S else "picked%d" % a
            words = keep.tile([P, b - a], U32, name="picked_words%d" % a, tag=tag, align_bytes=64)
            nc.vector.tensor_copy(words[:], x_table[:].indirect(entries(offs_t, a, b)))
            picked.append(words)
        w1_planes.append(quantise_weight(other_rounded[:, :1], P, "w1_second", "w1_second") + (0,))
        last_pair = quantise_weight(other_rounded[:, 1:], 2 * P, "w1_last", "w1_last")
        w1_planes.extend([last_pair + (0,), last_pair + (P,)])

        y = [keep.tile([P, S], F32, name="y%d" % t) for t in range(PACK)]
        for t, (w1_codes, w1_scales, start) in enumerate(w1_planes):
            cols = slice(start, start + P)
            for n, (a, b) in enumerate(spans(FIRST_PLANE_BANKS if t == 0 else (BANK, BANK))):
                bank = psum.tile([P, b - a], F32, name="bank")
                for words, (c, d) in zip(picked, spans(PICK_PIECES)):
                    lo, hi = max(a, c), min(b, d)
                    if lo < hi:
                        nc.tensor.matmul_mx(
                            bank[:, lo - a : hi - a],
                            w1_codes[:, cols].bitcast(FP8X4),
                            w1_scales[:, cols],
                            words[:, lo - c : hi - c].bitcast(FP8X4),
                            picked_scales[:, lo:hi],
                            start=True,
                            stop=True,
                        )
                relu(y[t][:, a:b], bank[:], t == 0 and n in (0, 2))

        pieces = spans(FINE_PIECES)
        fused = (pieces[0][0], pieces[1][1])
        y_all = {}
        for name, (a, b) in (("y_head", pieces[2]), ("y_tail", (pieces[3][0], S))):
            y_all[a] = keep.tile([P, PACK, b - a], F32, name=name, align_bytes=64)
            for t in range(PACK):
                nc.sync.dma_start(y_all[a][:, t, :], y[t][:, a:b])

        def gather(out, window, offsets, on_vector):
            if on_vector:
                nc.vector.tensor_copy(out, window.indirect(offsets))
            else:
                nc.scalar.activation(out, window.indirect(offsets), COPY)

        w2_high = load_weight_columns(w2, H // 2, (H // 2,), "w2_high", "raw_low")
        w2_front = keep.tile([P, 2, P, PACK], BF16, name="w2_front", align_bytes=64)
        for raw, start in ((w2_low, 0), (w2_high, P // 2)):
            nc.scalar.activation(dealt(w2_front[:, :, start : start + P // 2, :]), by_lines(raw)[:, :, :, :2], COPY)

        w3_raw = keep.tile([P, N], U32, name="w3_raw", tag="raw_high")
        nc.sync.dma_start(w3_raw[:].bitcast(I32), w3_words[0].rearrange("p n r -> p (n r)").bitcast(I32))
        w3_rows = load_scale_rows(w3_scales, N, "w3_rows")
        residual = {}
        freed = ("wide", "rounded", "w1_first", "w1_first_scales", "w1_second", "w1_second_scales", "picked0", "picked512", "w1_last", "picked_scales")
        for k, (a, b) in enumerate(pieces):
            for u in range(2):
                residual[k, u] = keep.tile([P, 2, b - a], F32, name="residual%d_%d" % (k, u), tag=freed[2 * k + u], align_bytes=64)
                nc.sync.dma_start(residual[k, u][:], res.rearrange("(p t) j -> p t j", t=PACK)[:, 2 * u : 2 * u + 2, a:b])

        pools = spans(POOL_PIECES)
        ordered = [keep.tile([P, PACK, b - a], BF16, name="ordered%d" % a, align_bytes=64) for a, b in pools]
        for t in (0, 1):
            for piece, (a, b) in zip(ordered, pools):
                gather(piece[:, t, :], y[t][:], entries(order_t, a, b), True)
        for piece, (a, b) in zip(ordered, pools):
            for t in (2, 3):
                gather(piece[:, t, :], y[t][:], entries(order_t, a, b), (a, t) == (0, 2))
        w2_pairs = [quantise_weight(w2_front[:], 2 * P, "w2_low", "w2_low")]

        def largest(n):
            a, b = pools[n]
            z = keep.tile([P, (b - a) // 2 * PACK], BF16, name="z%d" % n, align_bytes=64)
            members = ordered[n][:].rearrange("p t (c i e) -> p e c t i", i=LINE, e=2)
            nc.vector.tensor_tensor(z[:].rearrange("p (c i t) -> p c t i", i=LINE, t=PACK), members[:, 0], members[:, 1], MAX)
            return z

        z_codes = keep.tile([P, V], U32, name="z_codes", align_bytes=64)
        z_scales = keep.tile([P, V], U8, name="z_scales", align_bytes=64)

        def quantise_z(z, a, b):
            nc.vector.quantize_mx(z_codes[:, a // 2 : b // 2].bitcast(FP8X4), z_scales[:, a // 2 : b // 2], z[:])

        h = [keep.tile([P, 2 * V], F32, name="h%d" % t, align_bytes=64) for t in range(PACK)]

        def coarse_product(t, a, b, on_vector):
            w2_codes, w2_scales = w2_pairs[t // 2]
            cols = slice(t % 2 * P, (t % 2 + 1) * P)
            coarse = slice(a // 2, b // 2)
            bank = psum.tile([P, (b - a) // 2], F32, name="bank")
            nc.tensor.matmul_mx(
                bank[:],
                w2_codes[:, cols].bitcast(FP8X4),
                w2_scales[:, cols],
                z_codes[:, coarse].bitcast(FP8X4),
                z_scales[:, coarse],
                start=True,
                stop=True,
            )
            relu(h[t][:, coarse], bank[:], on_vector)

        first, second, last = pools
        z_first = largest(0)
        z_second = largest(1)
        quantise_z(z_first, *first)
        quantise_z(z_second, *second)
        z_last = largest(2)
        w3_codes = keep.tile([P, N], U32, name="w3_codes", tag="ordered%d" % second[0], align_bytes=64)
        nc.vector.tensor_copy(w3_codes[:].rearrange("p (t m) -> p m t", t=PACK), w3_raw[:].rearrange("p (m t) -> p m t", t=PACK))
        quantise_z(z_last, *last)

        w2_back = keep.tile([P, 2, P, PACK], BF16, name="w2_back", tag="ordered0", align_bytes=64)
        for raw, start in ((w2_low, 0), (w2_high, P // 2)):
            nc.scalar.activation(dealt(w2_back[:, :, start : start + P // 2, :]), by_lines(raw)[:, :, :, 2:], COPY)
        coarse_product(0, *first, False)
        w2_pairs.append(quantise_weight(w2_back[:], 2 * P, "w2_high", "w2_high"))
        w3_planes = keep.tile([P, N], U8, name="w3_planes", tag="z1", align_bytes=64)
        nc.vector.tensor_copy(w3_planes[:].rearrange("p (t m) -> p m t", t=PACK), w3_rows[:].rearrange("p (m t) -> p m t", t=PACK))
        coarse_product(0, *second, False)
        coarse_product(0, *last, False)
        for t in range(1, PACK):
            coarse_product(t, 0, S, False)

        out_rows = out_0.rearrange("(p t) j -> p t j", t=PACK)
        out_words = out_1[0].rearrange("p n r -> p (n r)").bitcast(I32)
        word_starts = {b: a for a, b in spans(WORD_PIECES)}

        def fetch(a, b, tag):
            fetched = keep.tile([P, PACK, b - a], F32, name="fetched%d" % a, tag=tag, align_bytes=64)
            for t in range(PACK):
                gather(fetched[:, t, :], h[t][:], entries(par_t, a, b), False)
            return fetched

        def add_fine(z2, fetched, a, b):
            start = max(begin for begin in y_all if begin <= a)
            nc.vector.tensor_tensor(
                z2.rearrange("p (c i t) -> p c t i", i=LINE, t=PACK),
                fetched[:, :, a - start : b - start].rearrange("p t (c i) -> p c t i", i=LINE),
                y_all[start][:, :, a - start : b - start].rearrange("p t (c i) -> p c t i", i=LINE),
                ADD,
            )

        def fine_product(k, z2, tag):
            a, b = pieces[k]
            width = b - a
            z2_codes = keep.tile([P, width], U32, name="z2_codes%d" % k, tag=tag, align_bytes=64)
            z2_scales = keep.tile([P, width], U8, name="z2_scales%d" % k, align_bytes=64)
            nc.vector.quantize_mx(z2_codes[:].bitcast(FP8X4), z2_scales[:], z2[:])
            per_bank = 2
            banks = []
            for t0 in range(0, PACK, per_bank):
                bank = psum.tile([P, per_bank, width], F32, name="bank")
                for i in range(per_bank):
                    cols = slice((t0 + i) * P, (t0 + i + 1) * P)
                    nc.tensor.matmul_mx(
                        bank[:, i, :],
                        w3_codes[:, cols].bitcast(FP8X4),
                        w3_planes[:, cols],
                        z2_codes[:].bitcast(FP8X4),
                        z2_scales[:],
                        start=True,
                        stop=True,
                    )
                banks.append((slice(t0, t0 + per_bank), bank))
            return banks

        def add_residual(k, banks):
            a, b = pieces[k]
            result = keep.tile([P, PACK, b - a], F32, name="result%d" % k, align_bytes=64)
            for u, (planes, bank) in enumerate(banks):
                nc.vector.tensor_tensor(result[:, planes, :], bank[:], residual[k, u][:], ADD)
                if k == 0:
                    nc.sync.dma_start(out_rows[:, planes, a:b], result[:, planes, :])
            if k != 0:
                nc.sync.dma_start(out_rows[:, :, a:b], result[:])
            return result

        sums = keep.tile([P, PACK, fused[1] - fused[0]], F32, name="sums", align_bytes=64)
        for t in range(PACK):
            for a, b in pieces[:2] if t == PACK - 1 else (fused,):
                nc.vector.tensor_tensor(sums[:, t, a:b], h[t][:].indirect(entries(par_t, a, b)), y[t][:, a:b], ADD)
        fetched = fetch(*pieces[2], "w2_low")
        z2 = {k: round_interleaved(sums[:, :, pieces[k][0] - fused[0] : pieces[k][1] - fused[0]], FINE_PIECES[k], "z2_rounded", 2, k == 0) for k in (0, 1)}
        a, b = pieces[2]
        z2[2] = keep.tile([P, (b - a) * PACK], BF16, name="z2_2", align_bytes=64)
        add_fine(z2[2][:, : (b - a) * 2], fetched, a, (a + b) // 2)
        banks = {0: fine_product(0, z2[0], "z2_codes0")}
        add_fine(z2[2][:, (b - a) * 2 :], fetched, (a + b) // 2, b)
        banks.update({k: fine_product(k, z2[k], "z2_codes%d" % k) for k in (1, 2)})
        fetched = fetch(pieces[3][0], S, "sums")
        results = [add_residual(k, banks[k]) for k in range(3)]
        for k, tag in ((3, freed[4]), (4, freed[3])):
            z2[k] = keep.tile([P, FINE_PIECES[k] * PACK], BF16, name="z2_%d" % k, tag=tag, align_bytes=64)
            add_fine(z2[k][:], fetched, *pieces[k])
        banks = {k: fine_product(k, z2[k], "z2_codes%d" % k) for k in (3, 4)}
        results.extend(add_residual(k, banks[k]) for k in (3, 4))

        out_scales = keep.tile([P, S], U8, name="out_scales", tag="sums", align_bytes=64)
        result_codes = keep.tile([P, S], U32, name="result_codes", align_bytes=64)
        for (a, b), result in zip(pieces, results):
            result_rounded = round_interleaved(result[:], b - a, "result_rounded", len(pieces), b == S)
            nc.vector.quantize_mx(result_codes[:, a:b].bitcast(FP8X4), out_scales[:, a:b], result_rounded[:])
            if b in word_starts:
                nc.sync.dma_start(out_words[:, word_starts[b] : b], result_codes[:, word_starts[b] : b].bitcast(I32))
        for q in range(QUADRANTS):
            queue = nc.sync if q < QUADRANTS // 2 else nc.scalar
            queue.dma_start(out_2[0, 4 * q : 4 * q + 4, :].bitcast(I32), out_scales[32 * q : 32 * q + 4, :].bitcast(I32))
